import numpy as np
import ml_dtypes


def mxq(x, axis, fmt="e4m3"):
    dtype, down = {"e4m3": (ml_dtypes.float8_e4m3fn, 7), "e5m2": (ml_dtypes.float8_e5m2, 14)}[fmt]
    v = np.moveaxis(np.asarray(x, np.float32).astype(ml_dtypes.bfloat16).astype(np.float64), axis, -1)
    blocks = v.reshape(v.shape[:-1] + (-1, 32))
    amax = np.abs(blocks).max(-1, keepdims=True)
    byte = np.maximum(np.where(amax > 0, np.frexp(amax)[1] - 1 + 127, 0) - down, 1)
    scale = np.exp2(byte - 127.0)
    codes = (blocks / scale).astype(np.float32).astype(dtype).astype(np.float64)
    return np.moveaxis((codes * scale).reshape(v.shape), -1, axis)


WIDE = False


def mx_kscale(k):
    if not WIDE:
        return np.ones(k)
    levels = np.array([10, -10, 5, -5, 0])
    if k % 512:
        return np.exp2(np.random.permutation(np.resize(levels, k // 32))).repeat(32)
    a = np.empty((k // 512, 16))
    for p in range(k // 512):
        a[p, :8] = np.random.permutation(np.resize(levels, 8))
        for g in range(8):
            far = levels[np.abs(levels - a[p, g]) >= 10]
            a[p, g + 8] = far[np.random.randint(len(far))]
    return np.exp2(a.ravel()).repeat(32)


def f64(x):
    return np.asarray(x).astype(np.float64)


def striped(idx):
    return np.tile(idx.reshape(-1, 16).T, (8, 1)).astype(np.uint16)


def unstriped(offs):
    return offs[:16].T.reshape(-1).astype(np.int64)


def striped8(idx):
    return np.concatenate([x.reshape(-1, 16).T for x in idx]).astype(np.uint16)


def runs(offs, k):
    lists = np.stack([offs[16 * r : 16 * r + 16].T.reshape(-1) for r in range(8)]).astype(np.int64)
    return lists[np.arange(k) % 512 // 64]


def pack_weight(w):
    k, n = w.shape
    w = f64(np.asarray(w, np.float32).astype(ml_dtypes.bfloat16)).reshape(k // 32, 32, n)
    amax = np.abs(w).max(1)
    byte = np.clip(np.where(amax > 0, np.frexp(amax)[1] - 1 + 127 - 7, 1), 1, 254)
    scaled = (w * np.exp2(127.0 - byte)[:, None, :]).reshape(k, n).astype(np.float32)
    words = np.ascontiguousarray(scaled.reshape(k // 512, 128, 4, n).transpose(0, 1, 3, 2)).astype(ml_dtypes.float8_e4m3fn).view(np.uint8)
    return words, np.ascontiguousarray(byte.astype(np.uint8).reshape(k // 512, 16, n))


def unpack_weight(words, scales):
    g, p, n, _ = words.shape
    vals = np.ascontiguousarray(words).view(ml_dtypes.float8_e4m3fn).astype(np.float64) * np.repeat(np.exp2(scales.astype(np.float64) - 127.0), 8, axis=1)[..., None]
    return vals.transpose(0, 1, 3, 2).reshape(g * 512, n)


K, T, S, N, H = 512, 2048, 512, 512, 512
P = 2 ** 7


def setup_inputs():
    n = np.random.standard_normal
    s = mx_kscale(K)[:, None]
    u = mx_kscale(H)
    packed_xT = pack_weight(n((K, T)) * s)
    return {
        "x_words": packed_xT[0],
        "x_scales": packed_xT[1],
        "w1": (n((K, H)) / np.sqrt(K) / s * u).astype(np.float32),
        "ga": np.tile(np.random.uniform(0.2, 1.0, S), (P, 1)).astype(np.float32),
        "w2": (n((H, N)) / np.sqrt(H) / u[:, None]).astype(np.float32),
        "offs": striped(np.random.permutation(T)[:S]),
        "p1": striped8(np.stack([np.random.permutation(S) for _ in range(8)])),
        "p2": striped8(np.stack([np.random.permutation(S) for _ in range(8)])),
        "q1": striped8(np.stack([np.random.permutation(S) for _ in range(8)])),
    }


def reference(x_words, x_scales, w1, ga, w2, offs, p1, p2, q1):
    xq = unpack_weight(x_words, x_scales)[:, unstriped(offs)]
    y = mxq(f64(w1), 0, "e4m3").T @ xq
    h = y + f64(ga)[:1] * (y[np.arange(H)[:, None], runs(p1, H)] + y[np.arange(H)[:, None], runs(p2, H)])
    z = h - (h[np.arange(H)[:, None], runs(q1, H)])
    return mxq(f64(w2), 0, "e4m3").T @ mxq(z, 0, "e4m3")

@@ -1,0 +1,193 @@
+from contextlib import ExitStack
+
+import concourse.mybir as mybir
+from concourse.masks import make_identity
+
+K, T, S, N, H = 512, 2048, 512, 512, 512
+FLOPS = 2 * K * H * S + 2 * H * N * S
+
+F32 = mybir.dt.float32
+BF16 = mybir.dt.bfloat16
+I32 = mybir.dt.int32
+U32 = mybir.dt.uint32
+U16 = mybir.dt.uint16
+U8 = mybir.dt.uint8
+FP8X4 = mybir.dt.float8_e4m3fn_x4
+MULT = mybir.AluOpType.mult
+SUBTRACT = mybir.AluOpType.subtract
+
+P = 128
+PACK = 4
+LIST_ROWS = 16
+Y_WINDOW = 1024
+CHUNKS = (128, 128, 128, 128)
+
+
+def tile_picked_twohop8_none_p_kernel(
+    tc, x_words, x_scales, w1, ga, w2, offs, p1, p2, q1, out
+):
+    nc = tc.nc
+    with ExitStack() as ctx:
+        lists = ctx.enter_context(tc.tile_pool(name="lists", bufs=1))
+        keep = ctx.enter_context(tc.tile_pool(name="keep", bufs=1))
+        psum = ctx.enter_context(tc.psum_pool(name="psum", bufs=6))
+        psum_turned = ctx.enter_context(tc.psum_pool(name="psum_turned", bufs=2))
+
+        def bank():
+            return psum.tile([P, S], F32, name="bank")
+
+        def entries(list_tile, cols):
+            return list_tile[:, cols.start // LIST_ROWS : cols.stop // LIST_ROWS]
+
+        offs_sb = lists.tile([P, S // LIST_ROWS], U16, name="offs_sb")
+        p1_sb = lists.tile([P, S // LIST_ROWS], U16, name="p1_sb")
+        p2_sb = lists.tile([P, S // LIST_ROWS], U16, name="p2_sb")
+        q1_sb = lists.tile([P, S // LIST_ROWS], U16, name="q1_sb")
+
+        w1_raw = keep.tile([P, PACK, H], F32, name="w1_raw", tag="w1_raw_then_ga")
+        x_table = keep.tile([P, T], I32, name="x_table", tag="x_table_then_w2_raw")
+        scale_table = keep.tile([P, T], U8, name="scale_table", tag="scale_table_then_w1_bf", align_bytes=64)
+
+        nc.vector.memset(scale_table[:].bitcast(I32), 0)
+        nc.sync.dma_start(offs_sb[:], offs)
+        nc.sync.dma_start(p1_sb[:], p1)
+        nc.sync.dma_start(w1_raw[:], w1.rearrange("(p j) c -> p j c", j=PACK))
+        for q in range(4):
+            nc.scalar.dma_start(
+                scale_table[32 * q : 32 * q + 4, :].bitcast(I32),
+                x_scales[0, 4 * q : 4 * q + 4, :].bitcast(I32),
+            )
+        nc.sync.dma_start(x_table[:], x_words[0].rearrange("p n t -> p (n t)").bitcast(I32))
+        nc.sync.dma_start(p2_sb[:], p2)
+        nc.sync.dma_start(q1_sb[:], q1)
+
+        identity = keep.tile([P, P], F32, name="identity")
+        make_identity(nc, identity[:])
+
+        x_scale = keep.tile([P, S], U8, name="x_scale", align_bytes=64)
+        nc.vector.tensor_copy(x_scale[:], scale_table[:].indirect(offs_sb[:]))
+
+        w1_bf = keep.tile([P, PACK * H], BF16, name="w1_bf", tag="scale_table_then_w1_bf", align_bytes=64)
+        nc.vector.tensor_scalar(
+            w1_bf[:].rearrange("p (t m j) -> p m j t", t=PACK, j=PACK),
+            w1_raw[:].rearrange("p j (m t) -> p m j t", t=PACK),
+            -1.0,
+            None,
+            MULT,
+        )
+        ga_sb = keep.tile([P, S], F32, name="ga_sb", tag="w1_raw_then_ga")
+        nc.sync.dma_start(ga_sb[:], ga)
+        w1_codes = keep.tile([P, H], U32, name="w1_codes", tag="w1_codes_then_w2_bf", align_bytes=64)
+        w1_scale = keep.tile([P, H], U8, name="w1_scale", align_bytes=64)
+        nc.vector.quantize_mx(w1_codes[:].bitcast(FP8X4), w1_scale[:], w1_bf[:])
+
+        x_codes = keep.tile([P, S], U32, name="x_codes", align_bytes=64)
+        halves = [slice(0, S // 2), slice(S // 2, S)]
+        for cols in halves:
+            nc.vector.tensor_copy(
+                x_codes[:, cols], x_table[:].bitcast(U32).indirect(entries(offs_sb, cols))
+            )
+
+        w2_raw = keep.tile([P, PACK, N], F32, name="w2_raw", tag="x_table_then_w2_raw")
+        nc.sync.dma_start(w2_raw[:], w2.rearrange("(p j) c -> p j c", j=PACK))
+
+        y = [keep.tile([P, Y_WINDOW], F32, name="y%d" % t) for t in range(PACK)]
+        for t in range(PACK):
+            features = slice(t * P, (t + 1) * P)
+            for cols in halves if t == 0 else [slice(0, S)]:
+                acc = bank()
+                nc.tensor.matmul_mx(
+                    acc[:, cols],
+                    lhsT=w1_codes[:, features].bitcast(FP8X4),
+                    lhsT_scale=w1_scale[:, features],
+                    rhs=x_codes[:, cols].bitcast(FP8X4),
+                    rhs_scale=x_scale[:, cols],
+                    start=True,
+                    stop=True,
+                )
+                nc.scalar.copy(y[t][:, cols], acc[:, cols])
+
+        blocks = [slice(b * P, (b + 1) * P) for b in range(S // P)]
+        h_window = [keep.tile([P, S], F32, name="h_window%d" % t) for t in range(PACK)]
+        h_plain = [keep.tile([P, S], F32, name="h_plain%d" % t) for t in range(PACK)]
+        w2_bf = keep.tile([P, N, PACK], BF16, name="w2_bf", tag="w1_codes_then_w2_bf", align_bytes=64)
+
+        def interleave(copy, dst, src):
+            copy(
+                dst.rearrange("p (c i) t -> p c t i", i=4),
+                src.rearrange("p t (c i) -> p c t i", i=4),
+            )
+
+        for cols in blocks:
+            interleave(nc.scalar.copy, w2_bf[:, cols, :], w2_raw[:, :, cols])
+
+        for t in range(PACK):
+            first = keep.tile([P, S], F32, name="first%d" % t)
+            second = keep.tile([P, S], F32, name="second%d" % t)
+            nc.vector.tensor_tensor(first[:], y[t][:].indirect(p1_sb[:]), ga_sb[:], MULT)
+            nc.vector.tensor_tensor(second[:], y[t][:].indirect(p2_sb[:]), ga_sb[:], MULT)
+            turned = psum_turned.tile([P, S], F32, name="turned")
+            terms = [y[t], first, second]
+            for n, term in enumerate(terms):
+                for cols in blocks:
+                    nc.tensor.matmul(
+                        turned[:, cols],
+                        lhsT=term[:, cols],
+                        rhs=identity[:],
+                        is_transpose=True,
+                        start=(n == 0 and cols is blocks[0]),
+                        stop=(n == len(terms) - 1 and cols is blocks[-1]),
+                    )
+            turned_sb = keep.tile([P, S], F32, name="turned_sb%d" % t)
+            nc.scalar.copy(turned_sb[:], turned[:])
+            back = bank()
+            for cols in blocks:
+                nc.tensor.transpose(back[:, cols], turned_sb[:, cols], identity[:])
+            nc.scalar.copy(h_window[t][:], back[:])
+            nc.scalar.copy(h_plain[t][:], back[:])
+
+        w2_codes = keep.tile([P, N], U32, name="w2_codes", align_bytes=64)
+        w2_scale = keep.tile([P, N], U8, name="w2_scale", align_bytes=64)
+        nc.vector.quantize_mx(
+            w2_codes[:].bitcast(FP8X4), w2_scale[:], w2_bf[:].rearrange("p n j -> p (n j)")
+        )
+
+        out_rows = out.rearrange("(b p) n -> p b n", p=P)
+        start = 0
+        for c, width in enumerate(CHUNKS):
+            cols = slice(start, start + width)
+            start = start + width
+            last = c == len(CHUNKS) - 1
+            z = keep.tile([P, PACK, width], F32, name="z%d" % c)
+            for t in range(PACK):
+                nc.vector.tensor_tensor(
+                    z[:, t, :],
+                    h_window[t][:].indirect(entries(q1_sb, cols)),
+                    h_plain[t][:, cols],
+                    SUBTRACT,
+                )
+            z_bf = keep.tile([P, width, PACK], BF16, name="z_bf%d" % c, align_bytes=64)
+            interleave(nc.vector.tensor_copy if last else nc.scalar.copy, z_bf[:], z[:])
+            z_codes = keep.tile([P, width], U32, name="z_codes%d" % c, align_bytes=64)
+            z_scale = keep.tile([P, width], U8, name="z_scale%d" % c, align_bytes=64)
+            nc.vector.quantize_mx(
+                z_codes[:].bitcast(FP8X4), z_scale[:], z_bf[:].rearrange("p n t -> p (n t)")
+            )
+            result = keep.tile([P, N // P, width], F32, name="result%d" % c)
+            for pair in range(2):
+                acc = bank()
+                for b in range(2):
+                    rows = blocks[2 * pair + b]
+                    nc.tensor.matmul_mx(
+                        acc[:, b * width : (b + 1) * width],
+                        lhsT=w2_codes[:, rows].bitcast(FP8X4),
+                        lhsT_scale=w2_scale[:, rows],
+                        rhs=z_codes[:].bitcast(FP8X4),
+                        rhs_scale=z_scale[:],
+                        start=True,
+                        stop=True,
+                    )
+                dst = result[:, 2 * pair : 2 * pair + 2, :].rearrange("p b n -> p (b n)")
+                copy = nc.vector.tensor_copy if pair == 1 else nc.scalar.copy
+                copy(dst, acc[:, : 2 * width])
+            nc.sync.dma_start(out_rows[:, :, cols], result[:])

@@ -44,21 +44,27 @@ def tile_picked_twohop8_none_p_kernel(
         p2_sb = lists.tile([P, S // LIST_ROWS], U16, name="p2_sb")
         q1_sb = lists.tile([P, S // LIST_ROWS], U16, name="q1_sb")
 
-        w1_raw = keep.tile([P, PACK, H], F32, name="w1_raw", tag="w1_raw_then_ga")
-        x_table = keep.tile([P, T], I32, name="x_table", tag="x_table_then_w2_raw")
+        w1_raw = keep.tile([P, PACK, H], F32, name="w1_raw")
+        x_table = keep.tile([P, T], I32, name="x_table")
+        ga_sb = keep.tile([P, S], F32, name="ga_sb")
+        w2_raw = keep.tile([P, PACK, N], F32, name="w2_raw")
         scale_table = keep.tile([P, T], U8, name="scale_table", tag="scale_table_then_w1_bf", align_bytes=64)
 
         nc.vector.memset(scale_table[:].bitcast(I32), 0)
         nc.sync.dma_start(offs_sb[:], offs)
-        nc.sync.dma_start(p1_sb[:], p1)
-        nc.sync.dma_start(w1_raw[:], w1.rearrange("(p j) c -> p j c", j=PACK))
+        w1_rows = w1.rearrange("(p j) c -> p j c", j=PACK)
+        nc.sync.dma_start(w1_raw[:, :2, :], w1_rows[:, :2, :])
         for q in range(4):
-            nc.scalar.dma_start(
+            nc.sync.dma_start(
                 scale_table[32 * q : 32 * q + 4, :].bitcast(I32),
                 x_scales[0, 4 * q : 4 * q + 4, :].bitcast(I32),
             )
+        nc.sync.dma_start(w1_raw[:, 2:, :], w1_rows[:, 2:, :])
         nc.sync.dma_start(x_table[:], x_words[0].rearrange("p n t -> p (n t)").bitcast(I32))
+        nc.sync.dma_start(p1_sb[:], p1)
+        nc.sync.dma_start(ga_sb[:], ga)
         nc.sync.dma_start(p2_sb[:], p2)
+        nc.sync.dma_start(w2_raw[:], w2.rearrange("(p j) c -> p j c", j=PACK))
         nc.sync.dma_start(q1_sb[:], q1)
 
         identity = keep.tile([P, P], F32, name="identity")
@@ -67,7 +73,7 @@ def tile_picked_twohop8_none_p_kernel(
         x_scale = keep.tile([P, S], U8, name="x_scale", align_bytes=64)
         nc.vector.tensor_copy(x_scale[:], scale_table[:].indirect(offs_sb[:]))
 
-        w1_bf = keep.tile([P, PACK * H], BF16, name="w1_bf", tag="scale_table_then_w1_bf", align_bytes=64)
+        w1_bf = keep.tile([P, PACK * H], BF16, name="w1_bf", align_bytes=64)
         nc.vector.tensor_scalar(
             w1_bf[:].rearrange("p (t m j) -> p m j t", t=PACK, j=PACK),
             w1_raw[:].rearrange("p j (m t) -> p m j t", t=PACK),
@@ -75,21 +81,16 @@ def tile_picked_twohop8_none_p_kernel(
             None,
             MULT,
         )
-        ga_sb = keep.tile([P, S], F32, name="ga_sb", tag="w1_raw_then_ga")
-        nc.sync.dma_start(ga_sb[:], ga)
         w1_codes = keep.tile([P, H], U32, name="w1_codes", tag="w1_codes_then_w2_bf", align_bytes=64)
         w1_scale = keep.tile([P, H], U8, name="w1_scale", align_bytes=64)
         nc.vector.quantize_mx(w1_codes[:].bitcast(FP8X4), w1_scale[:], w1_bf[:])
 
-        x_codes = keep.tile([P, S], U32, name="x_codes", align_bytes=64)
+        x_codes = keep.tile([P, S], U32, name="x_codes", tag="scale_table_then_w1_bf", align_bytes=64)
         halves = [slice(0, S // 2), slice(S // 2, S)]
         for cols in halves:
             nc.vector.tensor_copy(
                 x_codes[:, cols], x_table[:].bitcast(U32).indirect(entries(offs_sb, cols))
             )
-
-        w2_raw = keep.tile([P, PACK, N], F32, name="w2_raw", tag="x_table_then_w2_raw")
-        nc.sync.dma_start(w2_raw[:], w2.rearrange("(p j) c -> p j c", j=PACK))
 
         y = [keep.tile([P, Y_WINDOW], F32, name="y%d" % t) for t in range(PACK)]
         for t in range(PACK):
@@ -118,7 +119,7 @@ def tile_picked_twohop8_none_p_kernel(
                 src.rearrange("p t (c i) -> p c t i", i=4),
             )
 
-        for cols in blocks:
+        for cols in blocks[:2]:
             interleave(nc.scalar.copy, w2_bf[:, cols, :], w2_raw[:, :, cols])
 
         for t in range(PACK):
@@ -144,7 +145,15 @@ def tile_picked_twohop8_none_p_kernel(
             for cols in blocks:
                 nc.tensor.transpose(back[:, cols], turned_sb[:, cols], identity[:])
             nc.scalar.copy(h_window[t][:], back[:])
-            nc.scalar.copy(h_plain[t][:], back[:])
+            if t < 2:
+                nc.sync.dma_start(h_plain[t][:], h_window[t][:])
+                cols = blocks[2 + t]
+                interleave(nc.scalar.copy, w2_bf[:, cols, :], w2_raw[:, :, cols])
+            elif t == 2:
+                nc.scalar.copy(h_plain[t][:], back[:])
+            else:
+                for cols in blocks:
+                    nc.scalar.copy(h_plain[t][:, cols], back[:, cols])
 
         w2_codes = keep.tile([P, N], U32, name="w2_codes", align_bytes=64)
         w2_scale = keep.tile([P, N], U8, name="w2_scale", align_bytes=64)
@@ -158,7 +167,10 @@ def tile_picked_twohop8_none_p_kernel(
             cols = slice(start, start + width)
             start = start + width
             last = c == len(CHUNKS) - 1
-            z = keep.tile([P, PACK, width], F32, name="z%d" % c)
+            z = keep.tile(
+                [P, PACK, width], F32, name="z%d" % c, align_bytes=64,
+                tag="z_bf0_then_z3" if last else "z%d" % c,
+            )
             for t in range(PACK):
                 nc.vector.tensor_tensor(
                     z[:, t, :],
@@ -166,7 +178,7 @@ def tile_picked_twohop8_none_p_kernel(
                     h_plain[t][:, cols],
                     SUBTRACT,
                 )
-            z_bf = keep.tile([P, width, PACK], BF16, name="z_bf%d" % c, align_bytes=64)
+            z_bf = keep.tile([P, width, PACK], BF16, name="z_bf%d" % c, align_bytes=64, tag="z_bf0_then_z3" if c == 0 else "z_bf%d" % c)
             interleave(nc.vector.tensor_copy if last else nc.scalar.copy, z_bf[:], z[:])
             z_codes = keep.tile([P, width], U32, name="z_codes%d" % c, align_bytes=64)
             z_scale = keep.tile([P, width], U8, name="z_scale%d" % c, align_bytes=64)
@@ -188,6 +200,6 @@ def tile_picked_twohop8_none_p_kernel(
                         stop=True,
                     )
                 dst = result[:, 2 * pair : 2 * pair + 2, :].rearrange("p b n -> p (b n)")
-                copy = nc.vector.tensor_copy if pair == 1 else nc.scalar.copy
+                copy = nc.vector.tensor_copy if (pair == 1 and c >= 2) else nc.scalar.copy
                 copy(dst, acc[:, : 2 * width])
             nc.sync.dma_start(out_rows[:, :, cols], result[:])

@@ -15,12 +15,13 @@ U8 = mybir.dt.uint8
 FP8X4 = mybir.dt.float8_e4m3fn_x4
 MULT = mybir.AluOpType.mult
 SUBTRACT = mybir.AluOpType.subtract
+ADD = mybir.AluOpType.add
 
 P = 128
 PACK = 4
 LIST_ROWS = 16
 Y_WINDOW = 1024
-CHUNKS = (128, 128, 128, 128)
+CHUNKS = (slice(0, 256), slice(256, 384), slice(384, 512))
 
 
 def tile_picked_twohop8_none_p_kernel(
@@ -44,7 +45,7 @@ def tile_picked_twohop8_none_p_kernel(
         p2_sb = lists.tile([P, S // LIST_ROWS], U16, name="p2_sb")
         q1_sb = lists.tile([P, S // LIST_ROWS], U16, name="q1_sb")
 
-        w1_raw = keep.tile([P, PACK, H], F32, name="w1_raw")
+        w1_raw = [keep.tile([P, PACK, H // 2], F32, name="w1_raw%d" % u) for u in range(2)]
         x_table = keep.tile([P, T], I32, name="x_table")
         ga_sb = keep.tile([P, S], F32, name="ga_sb")
         w2_raw = keep.tile([P, PACK, N], F32, name="w2_raw")
@@ -53,13 +54,13 @@ def tile_picked_twohop8_none_p_kernel(
         nc.vector.memset(scale_table[:].bitcast(I32), 0)
         nc.sync.dma_start(offs_sb[:], offs)
         w1_rows = w1.rearrange("(p j) c -> p j c", j=PACK)
-        nc.sync.dma_start(w1_raw[:, :2, :], w1_rows[:, :2, :])
+        nc.sync.dma_start(w1_raw[0][:], w1_rows[:, :, : H // 2])
         for q in range(4):
             nc.sync.dma_start(
                 scale_table[32 * q : 32 * q + 4, :].bitcast(I32),
                 x_scales[0, 4 * q : 4 * q + 4, :].bitcast(I32),
             )
-        nc.sync.dma_start(w1_raw[:, 2:, :], w1_rows[:, 2:, :])
+        nc.sync.dma_start(w1_raw[1][:], w1_rows[:, :, H // 2 :])
         nc.sync.dma_start(x_table[:], x_words[0].rearrange("p n t -> p (n t)").bitcast(I32))
         nc.sync.dma_start(p1_sb[:], p1)
         nc.sync.dma_start(ga_sb[:], ga)
@@ -74,13 +75,15 @@ def tile_picked_twohop8_none_p_kernel(
         nc.vector.tensor_copy(x_scale[:], scale_table[:].indirect(offs_sb[:]))
 
         w1_bf = keep.tile([P, PACK * H], BF16, name="w1_bf", align_bytes=64)
-        nc.vector.tensor_scalar(
-            w1_bf[:].rearrange("p (t m j) -> p m j t", t=PACK, j=PACK),
-            w1_raw[:].rearrange("p j (m t) -> p m j t", t=PACK),
-            -1.0,
-            None,
-            MULT,
-        )
+        w1_dealt = w1_bf[:].rearrange("p (t m j) -> p m j t", t=PACK, j=PACK)
+        for u in range(2):
+            nc.vector.tensor_scalar(
+                w1_dealt[:, u * P // 2 : (u + 1) * P // 2],
+                w1_raw[u][:].rearrange("p j (m t) -> p m j t", t=PACK),
+                -1.0,
+                None,
+                MULT,
+            )
         w1_codes = keep.tile([P, H], U32, name="w1_codes", tag="w1_codes_then_w2_bf", align_bytes=64)
         w1_scale = keep.tile([P, H], U8, name="w1_scale", align_bytes=64)
         nc.vector.quantize_mx(w1_codes[:].bitcast(FP8X4), w1_scale[:], w1_bf[:])
@@ -110,7 +113,7 @@ def tile_picked_twohop8_none_p_kernel(
 
         blocks = [slice(b * P, (b + 1) * P) for b in range(S // P)]
         h_window = [keep.tile([P, S], F32, name="h_window%d" % t) for t in range(PACK)]
-        h_plain = [keep.tile([P, S], F32, name="h_plain%d" % t) for t in range(PACK)]
+        h_plain = [keep.tile([P, S], F32, name="h_plain%d" % t) for t in range(2)]
         w2_bf = keep.tile([P, N, PACK], BF16, name="w2_bf", tag="w1_codes_then_w2_bf", align_bytes=64)
 
         def interleave(copy, dst, src):
@@ -122,13 +125,16 @@ def tile_picked_twohop8_none_p_kernel(
         for cols in blocks[:2]:
             interleave(nc.scalar.copy, w2_bf[:, cols, :], w2_raw[:, :, cols])
 
-        for t in range(PACK):
+        def neighbours(t):
             first = keep.tile([P, S], F32, name="first%d" % t)
             second = keep.tile([P, S], F32, name="second%d" % t)
             nc.vector.tensor_tensor(first[:], y[t][:].indirect(p1_sb[:]), ga_sb[:], MULT)
             nc.vector.tensor_tensor(second[:], y[t][:].indirect(p2_sb[:]), ga_sb[:], MULT)
+            return first, second
+
+        for t in range(PACK - 1):
+            terms = [y[t], *neighbours(t)]
             turned = psum_turned.tile([P, S], F32, name="turned")
-            terms = [y[t], first, second]
             for n, term in enumerate(terms):
                 for cols in blocks:
                     nc.tensor.matmul(
@@ -139,7 +145,7 @@ def tile_picked_twohop8_none_p_kernel(
                         start=(n == 0 and cols is blocks[0]),
                         stop=(n == len(terms) - 1 and cols is blocks[-1]),
                     )
-            turned_sb = keep.tile([P, S], F32, name="turned_sb%d" % t)
+            turned_sb = keep.tile([P, S], F32, name="turned_sb%d" % t, tag="turned_sb%d" % t)
             nc.scalar.copy(turned_sb[:], turned[:])
             back = bank()
             for cols in blocks:
@@ -149,36 +155,40 @@ def tile_picked_twohop8_none_p_kernel(
                 nc.sync.dma_start(h_plain[t][:], h_window[t][:])
                 cols = blocks[2 + t]
                 interleave(nc.scalar.copy, w2_bf[:, cols, :], w2_raw[:, :, cols])
-            elif t == 2:
-                nc.scalar.copy(h_plain[t][:], back[:])
-            else:
-                for cols in blocks:
-                    nc.scalar.copy(h_plain[t][:, cols], back[:, cols])
 
+        first, second = neighbours(PACK - 1)
+        partial = keep.tile([P, S], F32, name="partial")
+        nc.vector.tensor_tensor(partial[:], first[:], y[PACK - 1][:, :S], ADD)
         w2_codes = keep.tile([P, N], U32, name="w2_codes", align_bytes=64)
         w2_scale = keep.tile([P, N], U8, name="w2_scale", align_bytes=64)
         nc.vector.quantize_mx(
             w2_codes[:].bitcast(FP8X4), w2_scale[:], w2_bf[:].rearrange("p n j -> p (n j)")
         )
+        nc.vector.tensor_tensor(h_window[PACK - 1][:], partial[:], second[:], ADD)
 
+        plain3 = keep.tile([P, S], F32, name="plain3", tag="turned_sb2")
         out_rows = out.rearrange("(b p) n -> p b n", p=P)
-        start = 0
-        for c, width in enumerate(CHUNKS):
-            cols = slice(start, start + width)
-            start = start + width
+        for c, cols in enumerate(CHUNKS):
             last = c == len(CHUNKS) - 1
-            z = keep.tile(
-                [P, PACK, width], F32, name="z%d" % c, align_bytes=64,
-                tag="z_bf0_then_z3" if last else "z%d" % c,
+            width = cols.stop - cols.start
+            nc.scalar.copy(plain3[:, cols], h_window[3][:, cols])
+            plain2 = keep.tile(
+                [P, width], F32, name="plain2_%d" % c, align_bytes=64,
+                tag="hold1" if c == 0 else "plain2_%d" % c,
             )
-            for t in range(PACK):
+            nc.scalar.copy(plain2[:], h_window[2][:, cols])
+            plain = [h_plain[0][:, cols], h_plain[1][:, cols], plain2[:], plain3[:, cols]]
+            z = keep.tile([P, PACK, width], F32, name="z%d" % c, align_bytes=64, tag="hold%d" % c)
+            for t in (0, 1, 3, 2):
                 nc.vector.tensor_tensor(
                     z[:, t, :],
                     h_window[t][:].indirect(entries(q1_sb, cols)),
-                    h_plain[t][:, cols],
+                    plain[t],
                     SUBTRACT,
                 )
-            z_bf = keep.tile([P, width, PACK], BF16, name="z_bf%d" % c, align_bytes=64, tag="z_bf0_then_z3" if c == 0 else "z_bf%d" % c)
+            z_bf = keep.tile(
+                [P, width, PACK], BF16, name="z_bf%d" % c, align_bytes=64, tag="hold%d" % (c + 2)
+            )
             interleave(nc.vector.tensor_copy if last else nc.scalar.copy, z_bf[:], z[:])
             z_codes = keep.tile([P, width], U32, name="z_codes%d" % c, align_bytes=64)
             z_scale = keep.tile([P, width], U8, name="z_scale%d" % c, align_bytes=64)
@@ -200,6 +210,6 @@ def tile_picked_twohop8_none_p_kernel(
                         stop=True,
                     )
                 dst = result[:, 2 * pair : 2 * pair + 2, :].rearrange("p b n -> p (b n)")
-                copy = nc.vector.tensor_copy if (pair == 1 and c >= 2) else nc.scalar.copy
+                copy = nc.vector.tensor_copy if (pair == 1 and last) else nc.scalar.copy
                 copy(dst, acc[:, : 2 * width])
             nc.sync.dma_start(out_rows[:, :, cols], result[:])

@@ -48,47 +48,52 @@ def tile_picked_twohop8_none_p_kernel(
         w1_raw = [keep.tile([P, PACK, H // 2], F32, name="w1_raw%d" % u) for u in range(2)]
         x_table = keep.tile([P, T], I32, name="x_table")
         ga_sb = keep.tile([P, S], F32, name="ga_sb")
-        w2_raw = keep.tile([P, PACK, N], F32, name="w2_raw")
-        scale_table = keep.tile([P, T], U8, name="scale_table", tag="scale_table_then_w1_bf", align_bytes=64)
+        scale_table = keep.tile([P, T], U8, name="scale_table", tag="scale_table_then_w2_raw", align_bytes=64)
 
         nc.vector.memset(scale_table[:].bitcast(I32), 0)
-        nc.sync.dma_start(offs_sb[:], offs)
         w1_rows = w1.rearrange("(p j) c -> p j c", j=PACK)
         nc.sync.dma_start(w1_raw[0][:], w1_rows[:, :, : H // 2])
-        for q in range(4):
-            nc.sync.dma_start(
-                scale_table[32 * q : 32 * q + 4, :].bitcast(I32),
-                x_scales[0, 4 * q : 4 * q + 4, :].bitcast(I32),
-            )
+        nc.sync.dma_start(offs_sb[:], offs)
+        nc.sync.dma_start(scale_table[0:P:8, :].bitcast(I32), x_scales[0].bitcast(I32))
         nc.sync.dma_start(w1_raw[1][:], w1_rows[:, :, H // 2 :])
         nc.sync.dma_start(x_table[:], x_words[0].rearrange("p n t -> p (n t)").bitcast(I32))
         nc.sync.dma_start(p1_sb[:], p1)
         nc.sync.dma_start(ga_sb[:], ga)
         nc.sync.dma_start(p2_sb[:], p2)
-        nc.sync.dma_start(w2_raw[:], w2.rearrange("(p j) c -> p j c", j=PACK))
         nc.sync.dma_start(q1_sb[:], q1)
 
         identity = keep.tile([P, P], F32, name="identity")
         make_identity(nc, identity[:])
 
-        x_scale = keep.tile([P, S], U8, name="x_scale", align_bytes=64)
-        nc.vector.tensor_copy(x_scale[:], scale_table[:].indirect(offs_sb[:]))
-
         w1_bf = keep.tile([P, PACK * H], BF16, name="w1_bf", align_bytes=64)
         w1_dealt = w1_bf[:].rearrange("p (t m j) -> p m j t", t=PACK, j=PACK)
-        for u in range(2):
-            nc.vector.tensor_scalar(
-                w1_dealt[:, u * P // 2 : (u + 1) * P // 2],
-                w1_raw[u][:].rearrange("p j (m t) -> p m j t", t=PACK),
-                -1.0,
-                None,
-                MULT,
+        nc.scalar.mul(
+            w1_dealt[:, : P // 2], w1_raw[0][:].rearrange("p j (m t) -> p m j t", t=PACK), -1.0
+        )
+
+        picked_scale = keep.tile([P, S], U8, name="picked_scale", align_bytes=64)
+        nc.vector.tensor_copy(picked_scale[:], scale_table[:].indirect(offs_sb[:]))
+        x_scale = keep.tile([P, S], U8, name="x_scale", align_bytes=64)
+        nc.vector.tensor_copy(x_scale[:].bitcast(I32), picked_scale[:].bitcast(I32))
+        for j in range(1, PACK):
+            nc.scalar.dma_start(
+                x_scale[j:P:32, :].bitcast(I32), picked_scale[8 * j : P : 32, :].bitcast(I32)
             )
+        w2_raw = keep.tile([P, PACK, N], F32, name="w2_raw", tag="scale_table_then_w2_raw", align_bytes=64)
+        nc.sync.dma_start(w2_raw[:], w2.rearrange("(p j) c -> p j c", j=PACK))
+
+        nc.vector.tensor_scalar(
+            w1_dealt[:, P // 2 :],
+            w1_raw[1][:].rearrange("p j (m t) -> p m j t", t=PACK),
+            -1.0,
+            None,
+            MULT,
+        )
         w1_codes = keep.tile([P, H], U32, name="w1_codes", tag="w1_codes_then_w2_bf", align_bytes=64)
         w1_scale = keep.tile([P, H], U8, name="w1_scale", align_bytes=64)
         nc.vector.quantize_mx(w1_codes[:].bitcast(FP8X4), w1_scale[:], w1_bf[:])
 
-        x_codes = keep.tile([P, S], U32, name="x_codes", tag="scale_table_then_w1_bf", align_bytes=64)
+        x_codes = keep.tile([P, S], U32, name="x_codes", align_bytes=64)
         halves = [slice(0, S // 2), slice(S // 2, S)]
         for cols in halves:
             nc.vector.tensor_copy(

@@ -16,6 +16,7 @@ FP8X4 = mybir.dt.float8_e4m3fn_x4
 MULT = mybir.AluOpType.mult
 SUBTRACT = mybir.AluOpType.subtract
 ADD = mybir.AluOpType.add
+COPY = mybir.ActivationFunctionType.Copy
 
 P = 128
 PACK = 4
@@ -31,11 +32,10 @@ def tile_picked_twohop8_none_p_kernel(
     with ExitStack() as ctx:
         lists = ctx.enter_context(tc.tile_pool(name="lists", bufs=1))
         keep = ctx.enter_context(tc.tile_pool(name="keep", bufs=1))
-        psum = ctx.enter_context(tc.psum_pool(name="psum", bufs=6))
-        psum_turned = ctx.enter_context(tc.psum_pool(name="psum_turned", bufs=2))
+        psum = ctx.enter_context(tc.psum_pool(name="psum", bufs=1))
 
-        def bank():
-            return psum.tile([P, S], F32, name="bank")
+        def bank(b):
+            return psum.tile([P, S], F32, name="bank%d" % b)
 
         def entries(list_tile, cols):
             return list_tile[:, cols.start // LIST_ROWS : cols.stop // LIST_ROWS]
@@ -71,7 +71,7 @@ def tile_picked_twohop8_none_p_kernel(
             w1_dealt[:, : P // 2], w1_raw[0][:].rearrange("p j (m t) -> p m j t", t=PACK), -1.0
         )
 
-        picked_scale = keep.tile([P, S], U8, name="picked_scale", align_bytes=64)
+        picked_scale = keep.tile([P, S], U8, name="picked_scale", tag="picked_then_ga", align_bytes=64)
         nc.vector.tensor_copy(picked_scale[:], scale_table[:].indirect(offs_sb[:]))
         x_scale = keep.tile([P, S], U8, name="x_scale", align_bytes=64)
         nc.vector.tensor_copy(x_scale[:].bitcast(I32), picked_scale[:].bitcast(I32))
@@ -81,6 +81,9 @@ def tile_picked_twohop8_none_p_kernel(
             )
         w2_raw = keep.tile([P, PACK, N], F32, name="w2_raw", tag="scale_table_then_w2_raw", align_bytes=64)
         nc.sync.dma_start(w2_raw[:], w2.rearrange("(p j) c -> p j c", j=PACK))
+        ga_column = keep.tile([P, S // P], F32, name="ga_column", tag="picked_then_ga", align_bytes=64)
+        with nc.allow_non_contiguous_dma(reason="one weight a partition"):
+            nc.sync.dma_start(ga_column[:], ga[0].rearrange("(b p) -> p b", p=P))
 
         nc.vector.tensor_scalar(
             w1_dealt[:, P // 2 :],
@@ -101,10 +104,12 @@ def tile_picked_twohop8_none_p_kernel(
             )
 
         y = [keep.tile([P, Y_WINDOW], F32, name="y%d" % t) for t in range(PACK)]
+        first_banks = 0
         for t in range(PACK):
             features = slice(t * P, (t + 1) * P)
             for cols in halves if t == 0 else [slice(0, S)]:
-                acc = bank()
+                acc = bank(first_banks)
+                first_banks = first_banks + 1
                 nc.tensor.matmul_mx(
                     acc[:, cols],
                     lhsT=w1_codes[:, features].bitcast(FP8X4),
@@ -117,9 +122,16 @@ def tile_picked_twohop8_none_p_kernel(
                 nc.scalar.copy(y[t][:, cols], acc[:, cols])
 
         blocks = [slice(b * P, (b + 1) * P) for b in range(S // P)]
+        whole = slice(0, S)
         h_window = [keep.tile([P, S], F32, name="h_window%d" % t) for t in range(PACK)]
-        h_plain = [keep.tile([P, S], F32, name="h_plain%d" % t) for t in range(2)]
+        h_plain = [
+            [keep.tile([P, S // 2], F32, name="h_plain%d_%d" % (t, u)) for u in range(2)]
+            for t in range(3)
+        ]
         w2_bf = keep.tile([P, N, PACK], BF16, name="w2_bf", tag="w1_codes_then_w2_bf", align_bytes=64)
+        first = [keep.tile([P, S], F32, name="first%d" % t) for t in range(PACK)]
+        second = [keep.tile([P, S], F32, name="second%d" % t) for t in range(PACK)]
+        turned_sb = [keep.tile([P, S], F32, name="turned_sb%d" % t) for t in range(PACK)]
 
         def interleave(copy, dst, src):
             copy(
@@ -127,74 +139,158 @@ def tile_picked_twohop8_none_p_kernel(
                 src.rearrange("p t (c i) -> p c t i", i=4),
             )
 
-        for cols in blocks[:2]:
-            interleave(nc.scalar.copy, w2_bf[:, cols, :], w2_raw[:, :, cols])
+        def round_w2(b):
+            interleave(nc.scalar.copy, w2_bf[:, blocks[b], :], w2_raw[:, :, blocks[b]])
 
-        def neighbours(t):
-            first = keep.tile([P, S], F32, name="first%d" % t)
-            second = keep.tile([P, S], F32, name="second%d" % t)
-            nc.vector.tensor_tensor(first[:], y[t][:].indirect(p1_sb[:]), ga_sb[:], MULT)
-            nc.vector.tensor_tensor(second[:], y[t][:].indirect(p2_sb[:]), ga_sb[:], MULT)
-            return first, second
+        def inside(cols):
+            return [b for b in blocks if cols.start <= b.start and b.stop <= cols.stop]
 
-        for t in range(PACK - 1):
-            terms = [y[t], *neighbours(t)]
-            turned = psum_turned.tile([P, S], F32, name="turned")
-            for n, term in enumerate(terms):
-                for cols in blocks:
-                    nc.tensor.matmul(
-                        turned[:, cols],
-                        lhsT=term[:, cols],
-                        rhs=identity[:],
-                        is_transpose=True,
-                        start=(n == 0 and cols is blocks[0]),
-                        stop=(n == len(terms) - 1 and cols is blocks[-1]),
-                    )
-            turned_sb = keep.tile([P, S], F32, name="turned_sb%d" % t, tag="turned_sb%d" % t)
-            nc.scalar.copy(turned_sb[:], turned[:])
-            back = bank()
-            for cols in blocks:
-                nc.tensor.transpose(back[:, cols], turned_sb[:, cols], identity[:])
-            nc.scalar.copy(h_window[t][:], back[:])
-            if t < 2:
-                nc.sync.dma_start(h_plain[t][:], h_window[t][:])
-                cols = blocks[2 + t]
-                interleave(nc.scalar.copy, w2_bf[:, cols, :], w2_raw[:, :, cols])
+        def turn(acc, term, cols, start=False, stop=False):
+            parts = inside(cols)
+            for b in parts:
+                nc.tensor.matmul(
+                    acc[:, b],
+                    lhsT=term[:, b],
+                    rhs=identity[:],
+                    is_transpose=True,
+                    start=(start and b is parts[0]),
+                    stop=(stop and b is parts[-1]),
+                )
 
-        first, second = neighbours(PACK - 1)
-        partial = keep.tile([P, S], F32, name="partial")
-        nc.vector.tensor_tensor(partial[:], first[:], y[PACK - 1][:, :S], ADD)
+        def turn_back(acc, turned, at, start, stop):
+            for n in range(2):
+                nc.tensor.matmul(
+                    acc[:, at + n * P : at + (n + 1) * P],
+                    lhsT=turned[:, blocks[n]],
+                    rhs=identity[:],
+                    is_transpose=True,
+                    start=(start and n == 0),
+                    stop=(stop and n == 1),
+                )
+
+        y_turned = keep.tile([P, S], F32, name="y_turned")
+        acc = bank(3)
+        for nodes in blocks:
+            nc.tensor.matmul_mx(
+                acc[:, nodes],
+                lhsT=x_codes[:, nodes].bitcast(FP8X4),
+                lhsT_scale=x_scale[:, nodes],
+                rhs=w1_codes[:, blocks[3]].bitcast(FP8X4),
+                rhs_scale=w1_scale[:, blocks[3]],
+                start=True,
+                stop=True,
+            )
+        nc.scalar.copy(y_turned[:], acc[:])
+
+        for t in range(3):
+            nc.vector.tensor_tensor(first[t][:], y[t][:].indirect(p1_sb[:]), ga_sb[:], MULT)
+            for cols in halves if t == 2 else [whole]:
+                nc.vector.tensor_tensor(
+                    second[t][:, cols], y[t][:].indirect(entries(p2_sb, cols)), ga_sb[:, cols], MULT
+                )
+        for cols in halves:
+            nc.vector.tensor_copy(first[3][:, cols], y[3][:].indirect(entries(p1_sb, cols)))
+        for cols in halves:
+            nc.vector.tensor_tensor(
+                second[3][:, cols], y[3][:].indirect(entries(p2_sb, cols)), first[3][:, cols], ADD
+            )
+
+        work = keep.tile([P, 1792], F32, name="work", align_bytes=64)
+        z_at = (0, 1024, 0)
+        plain3 = [work[:, 1088:1344], work[:, 1536:1792]]
+
+        for b in range(2):
+            round_w2(b)
+        def close_sum(acc, t, u):
+            turn(acc, second[t], halves[u], stop=True)
+            nc.scalar.copy(turned_sb[t][:, halves[u]], acc[:, halves[u]])
+
+        def back_beside(acc, t, u):
+            turn_back(acc, turned_sb[t][:, halves[u]], halves[1 - u].start, False, False)
+
+        def copy_beside(acc, t, u):
+            nc.scalar.copy(h_window[t][:, halves[u]], acc[:, halves[1 - u]])
+
+        def second_copy(t):
+            nc.scalar.copy(h_plain[t][0][:], h_window[t][:, halves[0]])
+            nc.sync.dma_start(h_plain[t][1][:], h_window[t][:, halves[1]])
+
+        sum0, sum1, back3 = [bank(5), bank(6)], [bank(7), bank(0)], [bank(4), bank(3)]
+        for u in range(2):
+            turn(sum0[u], y[0], halves[u], start=True)
+        for u in range(2):
+            turn(sum0[u], first[0], halves[u])
+        for u in range(2):
+            turn(sum1[u], y[1], halves[u], start=True)
+        for u in range(2):
+            close_sum(sum0[u], 0, u)
+        round_w2(2)
+        round_w2(3)
+        for u in range(2):
+            turn_back(back3[u], y_turned[:, halves[u]], 0, True, False)
+        for u in range(2):
+            turn(sum1[u], first[1], halves[u])
+        for u in range(2):
+            back_beside(sum1[u], 0, u)
+        for u in range(2):
+            close_sum(sum1[u], 1, u)
+        for u in range(2):
+            copy_beside(sum1[u], 0, u)
+        second_copy(0)
+
+        sum2 = [bank(6), bank(5)]
+        for u in range(2):
+            turn(sum2[u], y[2], halves[u], start=True)
+        turn(sum2[0], first[2], halves[0])
+        for u in range(2):
+            back_beside(sum2[u], 1, u)
+        turn(sum2[1], first[2], halves[1])
+        for u in range(2):
+            close_sum(sum2[u], 2, u)
+            copy_beside(sum2[u], 1, u)
+
+        for u in range(2):
+            back = bank(1 + u)
+            turn_back(back, turned_sb[2][:, halves[u]], 0, True, True)
+            nc.scalar.copy(h_window[2][:, halves[u]], back[:, halves[0]])
+        second_copy(1)
+        second_copy(2)
+        for u in range(2):
+            acc = bank((5, 1)[u])
+            turn(acc, second[3], halves[u], start=True, stop=True)
+            for part in inside(halves[u]):
+                n = part.start // P
+                nc.scalar.activation(
+                    turned_sb[3][:, part], acc[:, part], COPY, scale=ga_column[:, n : n + 1]
+                )
+        for u in range(2):
+            turn_back(back3[u], turned_sb[3][:, halves[u]], 0, False, True)
+            nc.scalar.copy(h_window[3][:, halves[u]], back3[u][:, halves[0]])
+            nc.scalar.copy(plain3[u], back3[u][:, halves[0]])
+
         w2_codes = keep.tile([P, N], U32, name="w2_codes", align_bytes=64)
         w2_scale = keep.tile([P, N], U8, name="w2_scale", align_bytes=64)
-        nc.vector.quantize_mx(
-            w2_codes[:].bitcast(FP8X4), w2_scale[:], w2_bf[:].rearrange("p n j -> p (n j)")
-        )
-        nc.vector.tensor_tensor(h_window[PACK - 1][:], partial[:], second[:], ADD)
 
-        plain3 = keep.tile([P, S], F32, name="plain3", tag="turned_sb2")
         out_rows = out.rearrange("(b p) n -> p b n", p=P)
         for c, cols in enumerate(CHUNKS):
             last = c == len(CHUNKS) - 1
             width = cols.stop - cols.start
-            nc.scalar.copy(plain3[:, cols], h_window[3][:, cols])
-            plain2 = keep.tile(
-                [P, width], F32, name="plain2_%d" % c, align_bytes=64,
-                tag="hold1" if c == 0 else "plain2_%d" % c,
-            )
-            nc.scalar.copy(plain2[:], h_window[2][:, cols])
-            plain = [h_plain[0][:, cols], h_plain[1][:, cols], plain2[:], plain3[:, cols]]
-            z = keep.tile([P, PACK, width], F32, name="z%d" % c, align_bytes=64, tag="hold%d" % c)
-            for t in (0, 1, 3, 2):
+            z = work[:, z_at[c] : z_at[c] + PACK * width].rearrange("p (t c) -> p t c", t=PACK)
+            in_half = slice(cols.start % 256, (cols.stop - 1) % 256 + 1)
+            plain = [halved[cols.start // 256][:, in_half] for halved in h_plain + [plain3]]
+            for t in (0, 1, 2, 3) if c == 0 else (3, 0, 1, 2):
+                if c == 0 and t == 2:
+                    nc.vector.quantize_mx(
+                        w2_codes[:].bitcast(FP8X4), w2_scale[:], w2_bf[:].rearrange("p n j -> p (n j)")
+                    )
                 nc.vector.tensor_tensor(
                     z[:, t, :],
                     h_window[t][:].indirect(entries(q1_sb, cols)),
                     plain[t],
                     SUBTRACT,
                 )
-            z_bf = keep.tile(
-                [P, width, PACK], BF16, name="z_bf%d" % c, align_bytes=64, tag="hold%d" % (c + 2)
-            )
-            interleave(nc.vector.tensor_copy if last else nc.scalar.copy, z_bf[:], z[:])
+            z_bf = keep.tile([P, width, PACK], BF16, name="z_bf%d" % c, align_bytes=64)
+            interleave(nc.vector.tensor_copy if last else nc.scalar.copy, z_bf[:], z)
             z_codes = keep.tile([P, width], U32, name="z_codes%d" % c, align_bytes=64)
             z_scale = keep.tile([P, width], U8, name="z_scale%d" % c, align_bytes=64)
             nc.vector.quantize_mx(
@@ -202,7 +298,7 @@ def tile_picked_twohop8_none_p_kernel(
             )
             result = keep.tile([P, N // P, width], F32, name="result%d" % c)
             for pair in range(2):
-                acc = bank()
+                acc = bank((7, 0, 6, 2, 5, 1)[2 * c + pair])
                 for b in range(2):
                     rows = blocks[2 * pair + b]
                     nc.tensor.matmul_mx(

@@ -22,7 +22,6 @@ P = 128
 PACK = 4
 LIST_ROWS = 16
 Y_WINDOW = 1024
-CHUNKS = (slice(0, 256), slice(256, 384), slice(384, 512))
 
 
 def tile_picked_twohop8_none_p_kernel(
@@ -45,10 +44,12 @@ def tile_picked_twohop8_none_p_kernel(
         p2_sb = lists.tile([P, S // LIST_ROWS], U16, name="p2_sb")
         q1_sb = lists.tile([P, S // LIST_ROWS], U16, name="q1_sb")
 
-        w1_raw = [keep.tile([P, PACK, H // 2], F32, name="w1_raw%d" % u) for u in range(2)]
+        w1_raw = [
+            keep.tile([P, PACK, H // 2], F32, name="w1_raw%d" % u, tag=tag)
+            for u, tag in enumerate(("w1_raw0", "w1_raw_then_ga"))
+        ]
         x_table = keep.tile([P, T], I32, name="x_table")
-        ga_sb = keep.tile([P, S], F32, name="ga_sb")
-        scale_table = keep.tile([P, T], U8, name="scale_table", tag="scale_table_then_w2_raw", align_bytes=64)
+        scale_table = keep.tile([P, T], U8, name="scale_table", align_bytes=64)
 
         nc.vector.memset(scale_table[:].bitcast(I32), 0)
         w1_rows = w1.rearrange("(p j) c -> p j c", j=PACK)
@@ -58,14 +59,13 @@ def tile_picked_twohop8_none_p_kernel(
         nc.sync.dma_start(w1_raw[1][:], w1_rows[:, :, H // 2 :])
         nc.sync.dma_start(x_table[:], x_words[0].rearrange("p n t -> p (n t)").bitcast(I32))
         nc.sync.dma_start(p1_sb[:], p1)
-        nc.sync.dma_start(ga_sb[:], ga)
         nc.sync.dma_start(p2_sb[:], p2)
         nc.sync.dma_start(q1_sb[:], q1)
 
         identity = keep.tile([P, P], F32, name="identity")
         make_identity(nc, identity[:])
 
-        w1_bf = keep.tile([P, PACK * H], BF16, name="w1_bf", align_bytes=64)
+        w1_bf = keep.tile([P, PACK * H], BF16, name="w1_bf", tag="w1_bf_then_w2_raw", align_bytes=64)
         w1_dealt = w1_bf[:].rearrange("p (t m j) -> p m j t", t=PACK, j=PACK)
         nc.scalar.mul(
             w1_dealt[:, : P // 2], w1_raw[0][:].rearrange("p j (m t) -> p m j t", t=PACK), -1.0
@@ -76,14 +76,9 @@ def tile_picked_twohop8_none_p_kernel(
         x_scale = keep.tile([P, S], U8, name="x_scale", align_bytes=64)
         nc.vector.tensor_copy(x_scale[:].bitcast(I32), picked_scale[:].bitcast(I32))
         for j in range(1, PACK):
-            nc.scalar.dma_start(
+            nc.sync.dma_start(
                 x_scale[j:P:32, :].bitcast(I32), picked_scale[8 * j : P : 32, :].bitcast(I32)
             )
-        w2_raw = keep.tile([P, PACK, N], F32, name="w2_raw", tag="scale_table_then_w2_raw", align_bytes=64)
-        nc.sync.dma_start(w2_raw[:], w2.rearrange("(p j) c -> p j c", j=PACK))
-        ga_column = keep.tile([P, S // P], F32, name="ga_column", tag="picked_then_ga", align_bytes=64)
-        with nc.allow_non_contiguous_dma(reason="one weight a partition"):
-            nc.sync.dma_start(ga_column[:], ga[0].rearrange("(b p) -> p b", p=P))
 
         nc.vector.tensor_scalar(
             w1_dealt[:, P // 2 :],
@@ -92,9 +87,16 @@ def tile_picked_twohop8_none_p_kernel(
             None,
             MULT,
         )
+        ga_sb = keep.tile([P, S], F32, name="ga_sb", tag="w1_raw_then_ga")
+        nc.sync.dma_start(ga_sb[:], ga)
         w1_codes = keep.tile([P, H], U32, name="w1_codes", tag="w1_codes_then_w2_bf", align_bytes=64)
         w1_scale = keep.tile([P, H], U8, name="w1_scale", align_bytes=64)
         nc.vector.quantize_mx(w1_codes[:].bitcast(FP8X4), w1_scale[:], w1_bf[:])
+        w2_raw = keep.tile([P, PACK, N], F32, name="w2_raw", tag="w1_bf_then_w2_raw", align_bytes=64)
+        nc.sync.dma_start(w2_raw[:], w2.rearrange("(p j) c -> p j c", j=PACK))
+        ga_column = keep.tile([P, S // P], F32, name="ga_column", tag="picked_then_ga", align_bytes=64)
+        with nc.allow_non_contiguous_dma(reason="one weight a partition"):
+            nc.sync.dma_start(ga_column[:], ga[0].rearrange("(b p) -> p b", p=P))
 
         x_codes = keep.tile([P, S], U32, name="x_codes", align_bytes=64)
         halves = [slice(0, S // 2), slice(S // 2, S)]
@@ -123,10 +125,12 @@ def tile_picked_twohop8_none_p_kernel(
 
         blocks = [slice(b * P, (b + 1) * P) for b in range(S // P)]
         whole = slice(0, S)
-        h_window = [keep.tile([P, S], F32, name="h_window%d" % t) for t in range(PACK)]
-        h_plain = [
-            [keep.tile([P, S // 2], F32, name="h_plain%d_%d" % (t, u)) for u in range(2)]
-            for t in range(3)
+        h_window = [
+            keep.tile([P, Y_WINDOW if t == 0 else S], F32, name="h_window%d" % t) for t in range(PACK)
+        ]
+        plain0 = keep.tile([P, S], F32, name="plain0")
+        plain1, plain2 = [
+            [keep.tile([P, S // 2], F32, name="plain%d_%d" % (t, u)) for u in range(2)] for t in (1, 2)
         ]
         w2_bf = keep.tile([P, N, PACK], BF16, name="w2_bf", tag="w1_codes_then_w2_bf", align_bytes=64)
         first = [keep.tile([P, S], F32, name="first%d" % t) for t in range(PACK)]
@@ -184,20 +188,13 @@ def tile_picked_twohop8_none_p_kernel(
 
         for t in range(3):
             nc.vector.tensor_tensor(first[t][:], y[t][:].indirect(p1_sb[:]), ga_sb[:], MULT)
-            for cols in halves if t == 2 else [whole]:
-                nc.vector.tensor_tensor(
-                    second[t][:, cols], y[t][:].indirect(entries(p2_sb, cols)), ga_sb[:, cols], MULT
-                )
-        for cols in halves:
-            nc.vector.tensor_copy(first[3][:, cols], y[3][:].indirect(entries(p1_sb, cols)))
-        for cols in halves:
-            nc.vector.tensor_tensor(
-                second[3][:, cols], y[3][:].indirect(entries(p2_sb, cols)), first[3][:, cols], ADD
-            )
+            nc.vector.tensor_tensor(second[t][:], y[t][:].indirect(p2_sb[:]), ga_sb[:], MULT)
+        nc.vector.tensor_copy(first[3][:], y[3][:].indirect(p1_sb[:]))
+        nc.vector.tensor_tensor(second[3][:], y[3][:].indirect(p2_sb[:]), first[3][:], ADD)
 
-        work = keep.tile([P, 1792], F32, name="work", align_bytes=64)
-        z_at = (0, 1024, 0)
-        plain3 = [work[:, 1088:1344], work[:, 1536:1792]]
+        z = keep.tile([P, 5 * S], F32, name="z", align_bytes=64)
+        plain3_late = keep.tile([P, S // 2], F32, name="plain3_late")
+        plain3 = [z[:, 576:832], plain3_late[:]]
 
         for b in range(2):
             round_w2(b)
@@ -205,17 +202,7 @@ def tile_picked_twohop8_none_p_kernel(
             turn(acc, second[t], halves[u], stop=True)
             nc.scalar.copy(turned_sb[t][:, halves[u]], acc[:, halves[u]])
 
-        def back_beside(acc, t, u):
-            turn_back(acc, turned_sb[t][:, halves[u]], halves[1 - u].start, False, False)
-
-        def copy_beside(acc, t, u):
-            nc.scalar.copy(h_window[t][:, halves[u]], acc[:, halves[1 - u]])
-
-        def second_copy(t):
-            nc.scalar.copy(h_plain[t][0][:], h_window[t][:, halves[0]])
-            nc.sync.dma_start(h_plain[t][1][:], h_window[t][:, halves[1]])
-
-        sum0, sum1, back3 = [bank(5), bank(6)], [bank(7), bank(0)], [bank(4), bank(3)]
+        sum0, sum1 = [bank(5), bank(6)], [bank(7), bank(0)]
         for u in range(2):
             turn(sum0[u], y[0], halves[u], start=True)
         for u in range(2):
@@ -227,34 +214,47 @@ def tile_picked_twohop8_none_p_kernel(
         round_w2(2)
         round_w2(3)
         for u in range(2):
-            turn_back(back3[u], y_turned[:, halves[u]], 0, True, False)
-        for u in range(2):
             turn(sum1[u], first[1], halves[u])
         for u in range(2):
-            back_beside(sum1[u], 0, u)
+            turn_back(sum1[u], turned_sb[0][:, halves[u]], halves[1 - u].start, False, False)
         for u in range(2):
             close_sum(sum1[u], 1, u)
         for u in range(2):
-            copy_beside(sum1[u], 0, u)
-        second_copy(0)
+            nc.scalar.copy(h_window[0][:, halves[u]], sum1[u][:, halves[1 - u]])
+        nc.scalar.copy(plain0[:], h_window[0][:, whole])
 
         sum2 = [bank(6), bank(5)]
         for u in range(2):
             turn(sum2[u], y[2], halves[u], start=True)
         turn(sum2[0], first[2], halves[0])
+        back = bank(4)
+        turn_back(back, turned_sb[1][:, halves[0]], 0, True, True)
+        nc.scalar.copy(h_window[1][:, halves[0]], back[:, halves[0]])
+        nc.scalar.copy(plain1[0][:], back[:, halves[0]])
+        beside = [sum2[u][:, blocks[2 - 2 * u]] for u in range(2)]
         for u in range(2):
-            back_beside(sum2[u], 1, u)
+            nc.tensor.matmul(
+                beside[u],
+                lhsT=turned_sb[1][:, blocks[2 + u]],
+                rhs=identity[:],
+                is_transpose=True,
+                start=False,
+                stop=False,
+            )
         turn(sum2[1], first[2], halves[1])
         for u in range(2):
             close_sum(sum2[u], 2, u)
-            copy_beside(sum2[u], 1, u)
+            nc.scalar.copy(h_window[1][:, blocks[2 + u]], beside[u])
+        nc.sync.dma_start(plain1[1][:], h_window[1][:, halves[1]])
 
+        back3 = [bank(7), bank(0)]
+        for u in range(2):
+            turn_back(back3[u], y_turned[:, halves[u]], 0, True, False)
         for u in range(2):
             back = bank(1 + u)
             turn_back(back, turned_sb[2][:, halves[u]], 0, True, True)
             nc.scalar.copy(h_window[2][:, halves[u]], back[:, halves[0]])
-        second_copy(1)
-        second_copy(2)
+        nc.sync.dma_start(plain2[1][:], h_window[2][:, halves[1]])
         for u in range(2):
             acc = bank((5, 1)[u])
             turn(acc, second[3], halves[u], start=True, stop=True)
@@ -263,6 +263,8 @@ def tile_picked_twohop8_none_p_kernel(
                 nc.scalar.activation(
                     turned_sb[3][:, part], acc[:, part], COPY, scale=ga_column[:, n : n + 1]
                 )
+            if u == 0:
+                nc.scalar.copy(plain2[0][:], h_window[2][:, halves[0]])
         for u in range(2):
             turn_back(back3[u], turned_sb[3][:, halves[u]], 0, False, True)
             nc.scalar.copy(h_window[3][:, halves[u]], back3[u][:, halves[0]])
@@ -271,46 +273,71 @@ def tile_picked_twohop8_none_p_kernel(
         w2_codes = keep.tile([P, N], U32, name="w2_codes", align_bytes=64)
         w2_scale = keep.tile([P, N], U8, name="w2_scale", align_bytes=64)
 
+        def difference(dst, t, cols, plain):
+            nc.vector.tensor_tensor(dst, h_window[t][:].indirect(entries(q1_sb, cols)), plain, SUBTRACT)
+
+        def second_product(acc, codes, scale, rows):
+            nc.tensor.matmul_mx(
+                acc,
+                lhsT=w2_codes[:, rows].bitcast(FP8X4),
+                lhsT_scale=w2_scale[:, rows],
+                rhs=codes[:].bitcast(FP8X4),
+                rhs_scale=scale[:],
+                start=True,
+                stop=True,
+            )
+
         out_rows = out.rearrange("(b p) n -> p b n", p=P)
-        for c, cols in enumerate(CHUNKS):
-            last = c == len(CHUNKS) - 1
-            width = cols.stop - cols.start
-            z = work[:, z_at[c] : z_at[c] + PACK * width].rearrange("p (t c) -> p t c", t=PACK)
-            in_half = slice(cols.start % 256, (cols.stop - 1) % 256 + 1)
-            plain = [halved[cols.start // 256][:, in_half] for halved in h_plain + [plain3]]
-            for t in (0, 1, 2, 3) if c == 0 else (3, 0, 1, 2):
-                if c == 0 and t == 2:
-                    nc.vector.quantize_mx(
-                        w2_codes[:].bitcast(FP8X4), w2_scale[:], w2_bf[:].rearrange("p n j -> p (n j)")
-                    )
-                nc.vector.tensor_tensor(
-                    z[:, t, :],
-                    h_window[t][:].indirect(entries(q1_sb, cols)),
-                    plain[t],
-                    SUBTRACT,
-                )
-            z_bf = keep.tile([P, width, PACK], BF16, name="z_bf%d" % c, align_bytes=64)
-            interleave(nc.vector.tensor_copy if last else nc.scalar.copy, z_bf[:], z)
-            z_codes = keep.tile([P, width], U32, name="z_codes%d" % c, align_bytes=64)
-            z_scale = keep.tile([P, width], U8, name="z_scale%d" % c, align_bytes=64)
+
+        def rounded(b, copy, source):
+            z_bf = keep.tile([P, P, PACK], BF16, name="z_bf%d" % b, align_bytes=64)
+            copy(
+                z_bf[:].rearrange("p (c i) (a t) -> p c a t i", i=4, a=2),
+                source.rearrange("p a t (c i) -> p c a t i", i=4),
+            )
+            return z_bf
+
+        def finish(b, z_bf, banks):
+            z_codes = keep.tile([P, P], U32, name="z_codes%d" % b, align_bytes=64)
+            z_scale = keep.tile([P, P], U8, name="z_scale%d" % b, align_bytes=64)
             nc.vector.quantize_mx(
                 z_codes[:].bitcast(FP8X4), z_scale[:], z_bf[:].rearrange("p n t -> p (n t)")
             )
-            result = keep.tile([P, N // P, width], F32, name="result%d" % c)
-            for pair in range(2):
-                acc = bank((7, 0, 6, 2, 5, 1)[2 * c + pair])
-                for b in range(2):
-                    rows = blocks[2 * pair + b]
-                    nc.tensor.matmul_mx(
-                        acc[:, b * width : (b + 1) * width],
-                        lhsT=w2_codes[:, rows].bitcast(FP8X4),
-                        lhsT_scale=w2_scale[:, rows],
-                        rhs=z_codes[:].bitcast(FP8X4),
-                        rhs_scale=z_scale[:],
-                        start=True,
-                        stop=True,
-                    )
-                dst = result[:, 2 * pair : 2 * pair + 2, :].rearrange("p b n -> p (b n)")
-                copy = nc.vector.tensor_copy if (pair == 1 and last) else nc.scalar.copy
-                copy(dst, acc[:, : 2 * width])
-            nc.sync.dma_start(out_rows[:, :, cols], result[:])
+            result = keep.tile([P, N], F32, name="result%d" % b)
+            share = N // len(banks)
+            for n, at in enumerate(banks):
+                acc = bank(at)
+                cols = slice(n * share, (n + 1) * share)
+                for rows in inside(cols):
+                    second_product(acc[:, rows], z_codes, z_scale, rows)
+                copy = nc.vector.tensor_copy if n == 1 else nc.scalar.copy
+                copy(result[:, cols], acc[:, cols])
+                nc.sync.dma_start(
+                    out_rows[:, cols.start // P : cols.stop // P, blocks[b]],
+                    result[:, cols].rearrange("p (b n) -> p b n", n=P),
+                )
+
+        def planes(start, width, outer, inner):
+            span = z[:, start : start + 2 * outer * width]
+            return span.rearrange("p (a k c) -> p a k c", a=2, c=width)[:, :, 0 : inner + 1 : inner, :]
+
+        early, third = planes(0, 2 * P, 5, 4), planes(2 * P, P, 3, 2)
+        last = planes(3 * P, P, 5, 2).rearrange("p t a c -> p a t c")
+        late = [None, plain1[1], plain2[1], plain3[1]]
+
+        difference(z[:, whole], 0, whole, plain0[:])
+        difference(early[:, 0, 1, :], 1, halves[0], plain1[0][:])
+        nc.vector.quantize_mx(
+            w2_codes[:].bitcast(FP8X4), w2_scale[:], w2_bf[:].rearrange("p n j -> p (n j)")
+        )
+        difference(early[:, 1, 0, :], 2, halves[0], plain2[0][:])
+        difference(early[:, 1, 1, :], 3, halves[0], plain3[0])
+        for t in (3, 1, 2):
+            difference(third[:, t // 2, t % 2, :], t, blocks[2], late[t][:, blocks[0]])
+        finish(0, rounded(0, nc.scalar.copy, early[:, :, :, blocks[0]]), [3])
+        for t in (3, 1):
+            difference(last[:, t // 2, t % 2, :], t, blocks[3], late[t][:, blocks[1]])
+        finish(1, rounded(1, nc.scalar.copy, early[:, :, :, blocks[1]]), [4])
+        finish(2, rounded(2, nc.scalar.copy, third), [6])
+        difference(last[:, 1, 0, :], 2, blocks[3], late[2][:, blocks[1]])
+        finish(3, rounded(3, nc.vector.tensor_copy, last), [2, 5])

@@ -105,7 +105,7 @@ def tile_picked_twohop8_none_p_kernel(
                 x_codes[:, cols], x_table[:].bitcast(U32).indirect(entries(offs_sb, cols))
             )
 
-        y = [keep.tile([P, Y_WINDOW], F32, name="y%d" % t) for t in range(PACK)]
+        y = [keep.tile([P, Y_WINDOW if t < 3 else S], F32, name="y%d" % t) for t in range(PACK)]
         first_banks = 0
         for t in range(PACK):
             features = slice(t * P, (t + 1) * P)
@@ -188,9 +188,17 @@ def tile_picked_twohop8_none_p_kernel(
 
         for t in range(3):
             nc.vector.tensor_tensor(first[t][:], y[t][:].indirect(p1_sb[:]), ga_sb[:], MULT)
-            nc.vector.tensor_tensor(second[t][:], y[t][:].indirect(p2_sb[:]), ga_sb[:], MULT)
-        nc.vector.tensor_copy(first[3][:], y[3][:].indirect(p1_sb[:]))
-        nc.vector.tensor_tensor(second[3][:], y[3][:].indirect(p2_sb[:]), first[3][:], ADD)
+            for cols in halves if t == 2 else [whole]:
+                nc.vector.tensor_tensor(
+                    second[t][:, cols], y[t][:].indirect(entries(p2_sb, cols)), ga_sb[:, cols], MULT
+                )
+        for cols in halves:
+            nc.vector.tensor_copy(first[3][:, cols], y[3][:].indirect(entries(p1_sb, cols)))
+        last_parts = [halves[0], blocks[2], blocks[3]]
+        for cols in last_parts:
+            nc.vector.tensor_tensor(
+                second[3][:, cols], y[3][:].indirect(entries(p2_sb, cols)), first[3][:, cols], ADD
+            )
 
         z = keep.tile([P, 5 * S], F32, name="z", align_bytes=64)
         plain3_late = keep.tile([P, S // 2], F32, name="plain3_late")
@@ -221,7 +229,7 @@ def tile_picked_twohop8_none_p_kernel(
             close_sum(sum1[u], 1, u)
         for u in range(2):
             nc.scalar.copy(h_window[0][:, halves[u]], sum1[u][:, halves[1 - u]])
-        nc.scalar.copy(plain0[:], h_window[0][:, whole])
+        nc.sync.dma_start(plain0[:], h_window[0][:, whole])
 
         sum2 = [bank(6), bank(5)]
         for u in range(2):
@@ -230,7 +238,7 @@ def tile_picked_twohop8_none_p_kernel(
         back = bank(4)
         turn_back(back, turned_sb[1][:, halves[0]], 0, True, True)
         nc.scalar.copy(h_window[1][:, halves[0]], back[:, halves[0]])
-        nc.scalar.copy(plain1[0][:], back[:, halves[0]])
+        nc.sync.dma_start(plain1[0][:], h_window[1][:, halves[0]])
         beside = [sum2[u][:, blocks[2 - 2 * u]] for u in range(2)]
         for u in range(2):
             nc.tensor.matmul(
@@ -247,24 +255,25 @@ def tile_picked_twohop8_none_p_kernel(
             nc.scalar.copy(h_window[1][:, blocks[2 + u]], beside[u])
         nc.sync.dma_start(plain1[1][:], h_window[1][:, halves[1]])
 
-        back3 = [bank(7), bank(0)]
+        back = bank(1)
+        turn_back(back, turned_sb[2][:, halves[0]], 0, True, True)
+        nc.scalar.copy(h_window[2][:, halves[0]], back[:, halves[0]])
+        nc.scalar.copy(plain2[0][:], h_window[2][:, halves[0]])
+        back3 = [bank(6), bank(0)]
         for u in range(2):
             turn_back(back3[u], y_turned[:, halves[u]], 0, True, False)
-        for u in range(2):
-            back = bank(1 + u)
-            turn_back(back, turned_sb[2][:, halves[u]], 0, True, True)
-            nc.scalar.copy(h_window[2][:, halves[u]], back[:, halves[0]])
+        back = bank(2)
+        turn_back(back, turned_sb[2][:, halves[1]], 0, True, True)
+        nc.scalar.copy(h_window[2][:, halves[1]], back[:, halves[0]])
         nc.sync.dma_start(plain2[1][:], h_window[2][:, halves[1]])
-        for u in range(2):
-            acc = bank((5, 1)[u])
-            turn(acc, second[3], halves[u], start=True, stop=True)
-            for part in inside(halves[u]):
+        for cols, at in zip(last_parts, (5, 1, 2)):
+            acc = bank(at)
+            turn(acc, second[3], cols, start=True, stop=True)
+            for part in inside(cols):
                 n = part.start // P
                 nc.scalar.activation(
                     turned_sb[3][:, part], acc[:, part], COPY, scale=ga_column[:, n : n + 1]
                 )
-            if u == 0:
-                nc.scalar.copy(plain2[0][:], h_window[2][:, halves[0]])
         for u in range(2):
             turn_back(back3[u], turned_sb[3][:, halves[u]], 0, False, True)
             nc.scalar.copy(h_window[3][:, halves[u]], back3[u][:, halves[0]])
@@ -325,11 +334,11 @@ def tile_picked_twohop8_none_p_kernel(
         last = planes(3 * P, P, 5, 2).rearrange("p t a c -> p a t c")
         late = [None, plain1[1], plain2[1], plain3[1]]
 
-        difference(z[:, whole], 0, whole, plain0[:])
-        difference(early[:, 0, 1, :], 1, halves[0], plain1[0][:])
         nc.vector.quantize_mx(
             w2_codes[:].bitcast(FP8X4), w2_scale[:], w2_bf[:].rearrange("p n j -> p (n j)")
         )
+        difference(z[:, whole], 0, whole, plain0[:])
+        difference(early[:, 0, 1, :], 1, halves[0], plain1[0][:])
         difference(early[:, 1, 0, :], 2, halves[0], plain2[0][:])
         difference(early[:, 1, 1, :], 3, halves[0], plain3[0])
         for t in (3, 1, 2):
@@ -338,6 +347,6 @@ def tile_picked_twohop8_none_p_kernel(
         for t in (3, 1):
             difference(last[:, t // 2, t % 2, :], t, blocks[3], late[t][:, blocks[1]])
         finish(1, rounded(1, nc.scalar.copy, early[:, :, :, blocks[1]]), [4])
-        finish(2, rounded(2, nc.scalar.copy, third), [6])
+        finish(2, rounded(2, nc.scalar.copy, third), [7])
         difference(last[:, 1, 0, :], 2, blocks[3], late[2][:, blocks[1]])
         finish(3, rounded(3, nc.vector.tensor_copy, last), [2, 5])

@@ -1,7 +1,6 @@
 from contextlib import ExitStack
 
 import concourse.mybir as mybir
-from concourse.masks import make_identity
 
 K, T, S, N, H = 512, 2048, 512, 512, 512
 FLOPS = 2 * K * H * S + 2 * H * N * S
@@ -21,7 +20,7 @@ COPY = mybir.ActivationFunctionType.Copy
 P = 128
 PACK = 4
 LIST_ROWS = 16
-Y_WINDOW = 1024
+WIDE = 1024
 
 
 def tile_picked_twohop8_none_p_kernel(
@@ -62,16 +61,13 @@ def tile_picked_twohop8_none_p_kernel(
         nc.sync.dma_start(p2_sb[:], p2)
         nc.sync.dma_start(q1_sb[:], q1)
 
-        identity = keep.tile([P, P], F32, name="identity")
-        make_identity(nc, identity[:])
-
         w1_bf = keep.tile([P, PACK * H], BF16, name="w1_bf", tag="w1_bf_then_w2_raw", align_bytes=64)
         w1_dealt = w1_bf[:].rearrange("p (t m j) -> p m j t", t=PACK, j=PACK)
-        nc.scalar.mul(
-            w1_dealt[:, : P // 2], w1_raw[0][:].rearrange("p j (m t) -> p m j t", t=PACK), -1.0
+        nc.scalar.activation(
+            w1_dealt[:, : P // 2], w1_raw[0][:].rearrange("p j (m t) -> p m j t", t=PACK), COPY
         )
 
-        picked_scale = keep.tile([P, S], U8, name="picked_scale", tag="picked_then_ga", align_bytes=64)
+        picked_scale = keep.tile([P, S], U8, name="picked_scale", align_bytes=64)
         nc.vector.tensor_copy(picked_scale[:], scale_table[:].indirect(offs_sb[:]))
         x_scale = keep.tile([P, S], U8, name="x_scale", align_bytes=64)
         nc.vector.tensor_copy(x_scale[:].bitcast(I32), picked_scale[:].bitcast(I32))
@@ -80,229 +76,145 @@ def tile_picked_twohop8_none_p_kernel(
                 x_scale[j:P:32, :].bitcast(I32), picked_scale[8 * j : P : 32, :].bitcast(I32)
             )
 
-        nc.vector.tensor_scalar(
-            w1_dealt[:, P // 2 :],
-            w1_raw[1][:].rearrange("p j (m t) -> p m j t", t=PACK),
-            -1.0,
-            None,
-            MULT,
+        nc.vector.tensor_copy(
+            w1_dealt[:, P // 2 :], w1_raw[1][:].rearrange("p j (m t) -> p m j t", t=PACK)
         )
         ga_sb = keep.tile([P, S], F32, name="ga_sb", tag="w1_raw_then_ga")
         nc.sync.dma_start(ga_sb[:], ga)
-        w1_codes = keep.tile([P, H], U32, name="w1_codes", tag="w1_codes_then_w2_bf", align_bytes=64)
+        w1_codes = keep.tile([P, H], U32, name="w1_codes", align_bytes=64)
         w1_scale = keep.tile([P, H], U8, name="w1_scale", align_bytes=64)
         nc.vector.quantize_mx(w1_codes[:].bitcast(FP8X4), w1_scale[:], w1_bf[:])
         w2_raw = keep.tile([P, PACK, N], F32, name="w2_raw", tag="w1_bf_then_w2_raw", align_bytes=64)
         nc.sync.dma_start(w2_raw[:], w2.rearrange("(p j) c -> p j c", j=PACK))
-        ga_column = keep.tile([P, S // P], F32, name="ga_column", tag="picked_then_ga", align_bytes=64)
-        with nc.allow_non_contiguous_dma(reason="one weight a partition"):
-            nc.sync.dma_start(ga_column[:], ga[0].rearrange("(b p) -> p b", p=P))
 
         x_codes = keep.tile([P, S], U32, name="x_codes", align_bytes=64)
         halves = [slice(0, S // 2), slice(S // 2, S)]
-        for cols in halves:
+        blocks = [slice(b * P, (b + 1) * P) for b in range(S // P)]
+        x_parts = [halves[0], blocks[2], blocks[3]]
+        for cols in x_parts:
             nc.vector.tensor_copy(
                 x_codes[:, cols], x_table[:].bitcast(U32).indirect(entries(offs_sb, cols))
             )
 
-        y = [keep.tile([P, Y_WINDOW if t < 3 else S], F32, name="y%d" % t) for t in range(PACK)]
-        first_banks = 0
-        for t in range(PACK):
-            features = slice(t * P, (t + 1) * P)
-            for cols in halves if t == 0 else [slice(0, S)]:
-                acc = bank(first_banks)
-                first_banks = first_banks + 1
-                nc.tensor.matmul_mx(
-                    acc[:, cols],
-                    lhsT=w1_codes[:, features].bitcast(FP8X4),
-                    lhsT_scale=w1_scale[:, features],
-                    rhs=x_codes[:, cols].bitcast(FP8X4),
-                    rhs_scale=x_scale[:, cols],
-                    start=True,
-                    stop=True,
-                )
-                nc.scalar.copy(y[t][:, cols], acc[:, cols])
-
-        blocks = [slice(b * P, (b + 1) * P) for b in range(S // P)]
         whole = slice(0, S)
-        h_window = [
-            keep.tile([P, Y_WINDOW if t == 0 else S], F32, name="h_window%d" % t) for t in range(PACK)
-        ]
-        plain0 = keep.tile([P, S], F32, name="plain0")
-        plain1, plain2 = [
-            [keep.tile([P, S // 2], F32, name="plain%d_%d" % (t, u)) for u in range(2)] for t in (1, 2)
-        ]
-        w2_bf = keep.tile([P, N, PACK], BF16, name="w2_bf", tag="w1_codes_then_w2_bf", align_bytes=64)
-        first = [keep.tile([P, S], F32, name="first%d" % t) for t in range(PACK)]
-        second = [keep.tile([P, S], F32, name="second%d" % t) for t in range(PACK)]
-        turned_sb = [keep.tile([P, S], F32, name="turned_sb%d" % t) for t in range(PACK)]
 
-        def interleave(copy, dst, src):
-            copy(
-                dst.rearrange("p (c i) t -> p c t i", i=4),
-                src.rearrange("p t (c i) -> p c t i", i=4),
-            )
-
-        def round_w2(b):
-            interleave(nc.scalar.copy, w2_bf[:, blocks[b], :], w2_raw[:, :, blocks[b]])
-
-        def inside(cols):
-            return [b for b in blocks if cols.start <= b.start and b.stop <= cols.stop]
-
-        def turn(acc, term, cols, start=False, stop=False):
-            parts = inside(cols)
-            for b in parts:
-                nc.tensor.matmul(
-                    acc[:, b],
-                    lhsT=term[:, b],
-                    rhs=identity[:],
-                    is_transpose=True,
-                    start=(start and b is parts[0]),
-                    stop=(stop and b is parts[-1]),
-                )
-
-        def turn_back(acc, turned, at, start, stop):
-            for n in range(2):
-                nc.tensor.matmul(
-                    acc[:, at + n * P : at + (n + 1) * P],
-                    lhsT=turned[:, blocks[n]],
-                    rhs=identity[:],
-                    is_transpose=True,
-                    start=(start and n == 0),
-                    stop=(stop and n == 1),
-                )
-
-        y_turned = keep.tile([P, S], F32, name="y_turned")
-        acc = bank(3)
-        for nodes in blocks:
+        def first_product(acc, t, cols):
             nc.tensor.matmul_mx(
-                acc[:, nodes],
-                lhsT=x_codes[:, nodes].bitcast(FP8X4),
-                lhsT_scale=x_scale[:, nodes],
-                rhs=w1_codes[:, blocks[3]].bitcast(FP8X4),
-                rhs_scale=w1_scale[:, blocks[3]],
+                acc[:, cols],
+                lhsT=w1_codes[:, blocks[t]].bitcast(FP8X4),
+                lhsT_scale=w1_scale[:, blocks[t]],
+                rhs=x_codes[:, cols].bitcast(FP8X4),
+                rhs_scale=x_scale[:, cols],
                 start=True,
                 stop=True,
             )
-        nc.scalar.copy(y_turned[:], acc[:])
 
-        for t in range(3):
-            nc.vector.tensor_tensor(first[t][:], y[t][:].indirect(p1_sb[:]), ga_sb[:], MULT)
-            for cols in halves if t == 2 else [whole]:
-                nc.vector.tensor_tensor(
-                    second[t][:, cols], y[t][:].indirect(entries(p2_sb, cols)), ga_sb[:, cols], MULT
-                )
-        for cols in halves:
-            nc.vector.tensor_copy(first[3][:, cols], y[3][:].indirect(entries(p1_sb, cols)))
-        last_parts = [halves[0], blocks[2], blocks[3]]
-        for cols in last_parts:
-            nc.vector.tensor_tensor(
-                second[3][:, cols], y[3][:].indirect(entries(p2_sb, cols)), first[3][:, cols], ADD
-            )
+        y = [keep.tile([P, WIDE], F32, name="y%d" % t) for t in range(PACK)]
 
-        z = keep.tile([P, 5 * S], F32, name="z", align_bytes=64)
-        plain3_late = keep.tile([P, S // 2], F32, name="plain3_late")
-        plain3 = [z[:, 576:832], plain3_late[:]]
-
-        for b in range(2):
-            round_w2(b)
-        def close_sum(acc, t, u):
-            turn(acc, second[t], halves[u], stop=True)
-            nc.scalar.copy(turned_sb[t][:, halves[u]], acc[:, halves[u]])
-
-        sum0, sum1 = [bank(5), bank(6)], [bank(7), bank(0)]
-        for u in range(2):
-            turn(sum0[u], y[0], halves[u], start=True)
-        for u in range(2):
-            turn(sum0[u], first[0], halves[u])
-        for u in range(2):
-            turn(sum1[u], y[1], halves[u], start=True)
-        for u in range(2):
-            close_sum(sum0[u], 0, u)
-        round_w2(2)
-        round_w2(3)
-        for u in range(2):
-            turn(sum1[u], first[1], halves[u])
-        for u in range(2):
-            turn_back(sum1[u], turned_sb[0][:, halves[u]], halves[1 - u].start, False, False)
-        for u in range(2):
-            close_sum(sum1[u], 1, u)
-        for u in range(2):
-            nc.scalar.copy(h_window[0][:, halves[u]], sum1[u][:, halves[1 - u]])
-        nc.sync.dma_start(plain0[:], h_window[0][:, whole])
-
-        sum2 = [bank(6), bank(5)]
-        for u in range(2):
-            turn(sum2[u], y[2], halves[u], start=True)
-        turn(sum2[0], first[2], halves[0])
-        back = bank(4)
-        turn_back(back, turned_sb[1][:, halves[0]], 0, True, True)
-        nc.scalar.copy(h_window[1][:, halves[0]], back[:, halves[0]])
-        nc.sync.dma_start(plain1[0][:], h_window[1][:, halves[0]])
-        beside = [sum2[u][:, blocks[2 - 2 * u]] for u in range(2)]
-        for u in range(2):
-            nc.tensor.matmul(
-                beside[u],
-                lhsT=turned_sb[1][:, blocks[2 + u]],
-                rhs=identity[:],
-                is_transpose=True,
-                start=False,
-                stop=False,
-            )
-        turn(sum2[1], first[2], halves[1])
-        for u in range(2):
-            close_sum(sum2[u], 2, u)
-            nc.scalar.copy(h_window[1][:, blocks[2 + u]], beside[u])
-        nc.sync.dma_start(plain1[1][:], h_window[1][:, halves[1]])
-
-        back = bank(1)
-        turn_back(back, turned_sb[2][:, halves[0]], 0, True, True)
-        nc.scalar.copy(h_window[2][:, halves[0]], back[:, halves[0]])
-        nc.scalar.copy(plain2[0][:], h_window[2][:, halves[0]])
-        back3 = [bank(6), bank(0)]
-        for u in range(2):
-            turn_back(back3[u], y_turned[:, halves[u]], 0, True, False)
-        back = bank(2)
-        turn_back(back, turned_sb[2][:, halves[1]], 0, True, True)
-        nc.scalar.copy(h_window[2][:, halves[1]], back[:, halves[0]])
-        nc.sync.dma_start(plain2[1][:], h_window[2][:, halves[1]])
-        for cols, at in zip(last_parts, (5, 1, 2)):
+        def make_y(t, cols, at, copy):
             acc = bank(at)
-            turn(acc, second[3], cols, start=True, stop=True)
-            for part in inside(cols):
-                n = part.start // P
-                nc.scalar.activation(
-                    turned_sb[3][:, part], acc[:, part], COPY, scale=ga_column[:, n : n + 1]
-                )
-        for u in range(2):
-            turn_back(back3[u], turned_sb[3][:, halves[u]], 0, False, True)
-            nc.scalar.copy(h_window[3][:, halves[u]], back3[u][:, halves[0]])
-            nc.scalar.copy(plain3[u], back3[u][:, halves[0]])
+            first_product(acc, t, cols)
+            copy(y[t][:, cols], acc[:, cols])
 
+        make_y(0, x_parts[0], 0, nc.scalar.copy)
+        make_y(1, halves[0], 1, nc.vector.tensor_copy)
+        make_y(0, x_parts[1], 2, nc.scalar.copy)
+        make_y(0, x_parts[2], 3, nc.scalar.copy)
+        make_y(1, halves[1], 4, nc.vector.tensor_copy)
+        make_y(2, whole, 5, nc.vector.tensor_copy)
+        make_y(3, whole, 6, nc.vector.tensor_copy)
+
+        shared = dict(align_bytes=64)
+        first = [
+            keep.tile([P, S], F32, name="first%d" % t, tag="first%d" % t, **shared) for t in range(PACK)
+        ]
+        both = [keep.tile([P, S], F32, name="both%d" % t) for t in range(PACK)]
+        weighted = [
+            keep.tile([P, S], F32, name="weighted%d" % t, tag="weighted%d" % t, **shared)
+            for t in range(PACK)
+        ]
+        h_all = keep.tile([P, PACK * S], F32, name="h_all")
+        h_window = [h_all] + [
+            keep.tile([P, WIDE if t < PACK - 1 else S], F32, name="h_window%d" % t)
+            for t in range(1, PACK)
+        ]
+        far = keep.tile([P, PACK * S], F32, name="far")
         w2_codes = keep.tile([P, N], U32, name="w2_codes", align_bytes=64)
         w2_scale = keep.tile([P, N], U8, name="w2_scale", align_bytes=64)
 
-        def difference(dst, t, cols, plain):
-            nc.vector.tensor_tensor(dst, h_window[t][:].indirect(entries(q1_sb, cols)), plain, SUBTRACT)
+        def plane(tile, t, cols=whole):
+            return tile[:, t * S + cols.start : t * S + cols.stop]
 
-        def second_product(acc, codes, scale, rows):
-            nc.tensor.matmul_mx(
-                acc,
-                lhsT=w2_codes[:, rows].bitcast(FP8X4),
-                lhsT_scale=w2_scale[:, rows],
-                rhs=codes[:].bitcast(FP8X4),
-                rhs_scale=scale[:],
-                start=True,
-                stop=True,
+        def fetch_first(t):
+            nc.scalar.activation(first[t][:], y[t][:].indirect(p1_sb[:]), COPY)
+
+        def fetch_second(t):
+            nc.vector.tensor_tensor(both[t][:], y[t][:].indirect(p2_sb[:]), first[t][:], ADD)
+
+        def weigh(t):
+            nc.vector.tensor_tensor(weighted[t][:], both[t][:], ga_sb[:], MULT)
+
+        def add_own(t):
+            nc.vector.tensor_tensor(h_window[t][:, whole], weighted[t][:], y[t][:, whole], ADD)
+
+        def fetch_far(t, cols):
+            nc.scalar.activation(plane(far, t, cols), h_window[t][:].indirect(entries(q1_sb, cols)), COPY)
+
+        def round_w2(u, tag):
+            w2_bf = keep.tile([P, N // 2, PACK], BF16, name="w2_bf%d" % u, tag=tag, **shared)
+            nc.scalar.copy(
+                w2_bf[:].rearrange("p (c i) t -> p c t i", i=4),
+                w2_raw[:, :, halves[u]].rearrange("p t (c i) -> p c t i", i=4),
             )
+            return w2_bf
+
+        def quantise_w2(u, w2_bf):
+            nc.vector.quantize_mx(
+                w2_codes[:, halves[u]].bitcast(FP8X4),
+                w2_scale[:, halves[u]],
+                w2_bf[:].rearrange("p n j -> p (n j)"),
+            )
+
+        for t in range(PACK):
+            fetch_first(t)
+
+        fetch_second(0)
+        fetch_second(1)
+        weigh(0)
+        fetch_second(2)
+        add_own(0)
+        w2_early = round_w2(0, "first0")
+        fetch_far(0, whole)
+        weigh(1)
+        weigh(2)
+        add_own(1)
+        nc.sync.dma_start(plane(h_all, 1), h_window[1][:, whole])
+        add_own(2)
+        nc.sync.dma_start(plane(h_all, 2), h_window[2][:, whole])
+        w2_late = round_w2(1, "weighted0")
+        fetch_far(1, whole)
+        fetch_far(2, whole)
+        fetch_second(3)
+        quantise_w2(0, w2_early)
+        weigh(3)
+        quantise_w2(1, w2_late)
+        add_own(3)
+        nc.vector.tensor_copy(plane(h_all, 3), h_window[3][:, whole])
+        for cols in blocks:
+            fetch_far(3, cols)
 
         out_rows = out.rearrange("(b p) n -> p b n", p=P)
 
-        def rounded(b, copy, source):
+        def by_fours(tile, cols):
+            return tile[:].rearrange("p (t c i) -> p c t i", t=PACK, i=4)[:, cols.start // 4 : cols.stop // 4]
+
+        def difference(b):
             z_bf = keep.tile([P, P, PACK], BF16, name="z_bf%d" % b, align_bytes=64)
-            copy(
-                z_bf[:].rearrange("p (c i) (a t) -> p c a t i", i=4, a=2),
-                source.rearrange("p a t (c i) -> p c a t i", i=4),
+            nc.vector.tensor_tensor(
+                z_bf[:].rearrange("p (c i) t -> p c t i", i=4),
+                by_fours(h_all, blocks[b]),
+                by_fours(far, blocks[b]),
+                SUBTRACT,
             )
             return z_bf
 
@@ -317,8 +229,16 @@ def tile_picked_twohop8_none_p_kernel(
             for n, at in enumerate(banks):
                 acc = bank(at)
                 cols = slice(n * share, (n + 1) * share)
-                for rows in inside(cols):
-                    second_product(acc[:, rows], z_codes, z_scale, rows)
+                for rows in blocks[cols.start // P : cols.stop // P]:
+                    nc.tensor.matmul_mx(
+                        acc[:, rows],
+                        lhsT=w2_codes[:, rows].bitcast(FP8X4),
+                        lhsT_scale=w2_scale[:, rows],
+                        rhs=z_codes[:].bitcast(FP8X4),
+                        rhs_scale=z_scale[:],
+                        start=True,
+                        stop=True,
+                    )
                 copy = nc.vector.tensor_copy if n == 1 else nc.scalar.copy
                 copy(result[:, cols], acc[:, cols])
                 nc.sync.dma_start(
@@ -326,27 +246,10 @@ def tile_picked_twohop8_none_p_kernel(
                     result[:, cols].rearrange("p (b n) -> p b n", n=P),
                 )
 
-        def planes(start, width, outer, inner):
-            span = z[:, start : start + 2 * outer * width]
-            return span.rearrange("p (a k c) -> p a k c", a=2, c=width)[:, :, 0 : inner + 1 : inner, :]
-
-        early, third = planes(0, 2 * P, 5, 4), planes(2 * P, P, 3, 2)
-        last = planes(3 * P, P, 5, 2).rearrange("p t a c -> p a t c")
-        late = [None, plain1[1], plain2[1], plain3[1]]
-
-        nc.vector.quantize_mx(
-            w2_codes[:].bitcast(FP8X4), w2_scale[:], w2_bf[:].rearrange("p n j -> p (n j)")
-        )
-        difference(z[:, whole], 0, whole, plain0[:])
-        difference(early[:, 0, 1, :], 1, halves[0], plain1[0][:])
-        difference(early[:, 1, 0, :], 2, halves[0], plain2[0][:])
-        difference(early[:, 1, 1, :], 3, halves[0], plain3[0])
-        for t in (3, 1, 2):
-            difference(third[:, t // 2, t % 2, :], t, blocks[2], late[t][:, blocks[0]])
-        finish(0, rounded(0, nc.scalar.copy, early[:, :, :, blocks[0]]), [3])
-        for t in (3, 1):
-            difference(last[:, t // 2, t % 2, :], t, blocks[3], late[t][:, blocks[1]])
-        finish(1, rounded(1, nc.scalar.copy, early[:, :, :, blocks[1]]), [4])
-        finish(2, rounded(2, nc.scalar.copy, third), [7])
-        difference(last[:, 1, 0, :], 2, blocks[3], late[2][:, blocks[1]])
-        finish(3, rounded(3, nc.vector.tensor_copy, last), [2, 5])
+        z_bf = [difference(0), difference(1)]
+        finish(0, z_bf[0], [7])
+        z_bf.append(difference(2))
+        finish(1, z_bf[1], [3])
+        z_bf.append(difference(3))
+        finish(2, z_bf[2], [2])
+        finish(3, z_bf[3], [0, 1])

@@ -45,9 +45,9 @@ def tile_picked_twohop8_none_p_kernel(
 
         w1_raw = [
             keep.tile([P, PACK, H // 2], F32, name="w1_raw%d" % u, tag=tag)
-            for u, tag in enumerate(("w1_raw0", "w1_raw_then_ga"))
+            for u, tag in enumerate(("w1_raw0", "w1_raw_then_w2_raw"))
         ]
-        x_table = keep.tile([P, T], I32, name="x_table")
+        x_table = keep.tile([P, T], I32, name="x_table", tag="x_table_then_w2_bf", align_bytes=64)
         scale_table = keep.tile([P, T], U8, name="scale_table", align_bytes=64)
 
         nc.vector.memset(scale_table[:].bitcast(I32), 0)
@@ -67,7 +67,7 @@ def tile_picked_twohop8_none_p_kernel(
             w1_dealt[:, : P // 2], w1_raw[0][:].rearrange("p j (m t) -> p m j t", t=PACK), COPY
         )
 
-        picked_scale = keep.tile([P, S], U8, name="picked_scale", align_bytes=64)
+        picked_scale = keep.tile([P, S], U8, name="picked_scale", tag="picked_then_ga", align_bytes=64)
         nc.vector.tensor_copy(picked_scale[:], scale_table[:].indirect(offs_sb[:]))
         x_scale = keep.tile([P, S], U8, name="x_scale", align_bytes=64)
         nc.vector.tensor_copy(x_scale[:].bitcast(I32), picked_scale[:].bitcast(I32))
@@ -79,13 +79,18 @@ def tile_picked_twohop8_none_p_kernel(
         nc.vector.tensor_copy(
             w1_dealt[:, P // 2 :], w1_raw[1][:].rearrange("p j (m t) -> p m j t", t=PACK)
         )
-        ga_sb = keep.tile([P, S], F32, name="ga_sb", tag="w1_raw_then_ga")
-        nc.sync.dma_start(ga_sb[:], ga)
+        w2_rows = w2.rearrange("(p j) c -> p j c", j=PACK)
+        w2_early = keep.tile([P, PACK, N // 2], F32, name="w2_early", tag="w1_raw_then_w2_raw")
+        nc.sync.dma_start(w2_early[:], w2_rows[:, :, : N // 2])
         w1_codes = keep.tile([P, H], U32, name="w1_codes", align_bytes=64)
         w1_scale = keep.tile([P, H], U8, name="w1_scale", align_bytes=64)
         nc.vector.quantize_mx(w1_codes[:].bitcast(FP8X4), w1_scale[:], w1_bf[:])
-        w2_raw = keep.tile([P, PACK, N], F32, name="w2_raw", tag="w1_bf_then_w2_raw", align_bytes=64)
-        nc.sync.dma_start(w2_raw[:], w2.rearrange("(p j) c -> p j c", j=PACK))
+        w2_late = keep.tile(
+            [P, PACK, N // 2], F32, name="w2_late", tag="w1_bf_then_w2_raw", align_bytes=64
+        )
+        nc.sync.dma_start(w2_late[:], w2_rows[:, :, N // 2 :])
+        ga_sb = keep.tile([P, S], F32, name="ga_sb", tag="picked_then_ga", align_bytes=64)
+        nc.sync.dma_start(ga_sb[:], ga)
 
         x_codes = keep.tile([P, S], U32, name="x_codes", align_bytes=64)
         halves = [slice(0, S // 2), slice(S // 2, S)]
@@ -134,9 +139,9 @@ def tile_picked_twohop8_none_p_kernel(
             for t in range(PACK)
         ]
         h_all = keep.tile([P, PACK * S], F32, name="h_all")
-        h_window = [h_all] + [
+        h_window = [
             keep.tile([P, WIDE if t < PACK - 1 else S], F32, name="h_window%d" % t)
-            for t in range(1, PACK)
+            for t in range(PACK)
         ]
         far = keep.tile([P, PACK * S], F32, name="far")
         w2_codes = keep.tile([P, N], U32, name="w2_codes", align_bytes=64)
@@ -151,39 +156,44 @@ def tile_picked_twohop8_none_p_kernel(
         def fetch_second(t):
             nc.vector.tensor_tensor(both[t][:], y[t][:].indirect(p2_sb[:]), first[t][:], ADD)
 
-        def weigh(t):
-            nc.vector.tensor_tensor(weighted[t][:], both[t][:], ga_sb[:], MULT)
+        def weigh(t, cols=whole):
+            nc.vector.tensor_tensor(weighted[t][:, cols], both[t][:, cols], ga_sb[:, cols], MULT)
 
-        def add_own(t):
-            nc.vector.tensor_tensor(h_window[t][:, whole], weighted[t][:], y[t][:, whole], ADD)
+        def add_own(t, cols=whole):
+            nc.vector.tensor_tensor(h_window[t][:, cols], weighted[t][:, cols], y[t][:, cols], ADD)
 
         def fetch_far(t, cols):
             nc.scalar.activation(plane(far, t, cols), h_window[t][:].indirect(entries(q1_sb, cols)), COPY)
 
-        def round_w2(u, tag):
-            w2_bf = keep.tile([P, N // 2, PACK], BF16, name="w2_bf%d" % u, tag=tag, **shared)
-            nc.scalar.copy(
-                w2_bf[:].rearrange("p (c i) t -> p c t i", i=4),
-                w2_raw[:, :, halves[u]].rearrange("p t (c i) -> p c t i", i=4),
-            )
-            return w2_bf
+        w2_bf = keep.tile([P, N, PACK], BF16, name="w2_bf", tag="x_table_then_w2_bf", align_bytes=64)
 
-        def quantise_w2(u, w2_bf):
+        def w2_block(b):
+            source = (w2_early, w2_late)[b // 2][:, :, blocks[b % 2]]
+            return (
+                w2_bf[:, blocks[b], :].rearrange("p (c i) t -> p c t i", i=4),
+                source.rearrange("p t (c i) -> p c t i", i=4),
+            )
+
+        def quantise_w2(u):
             nc.vector.quantize_mx(
                 w2_codes[:, halves[u]].bitcast(FP8X4),
                 w2_scale[:, halves[u]],
-                w2_bf[:].rearrange("p n j -> p (n j)"),
+                w2_bf[:, halves[u], :].rearrange("p n j -> p (n j)"),
             )
 
+        for b in range(3):
+            nc.gpsimd.tensor_scalar(*w2_block(b), 1.0, 0.0, MULT, ADD)
         for t in range(PACK):
             fetch_first(t)
+        second = keep.tile([P, S], F32, name="second")
+        nc.scalar.activation(second[:], y[3][:].indirect(p2_sb[:]), COPY)
 
         fetch_second(0)
         fetch_second(1)
         weigh(0)
         fetch_second(2)
         add_own(0)
-        w2_early = round_w2(0, "first0")
+        nc.sync.dma_start(plane(h_all, 0), h_window[0][:, whole])
         fetch_far(0, whole)
         weigh(1)
         weigh(2)
@@ -191,17 +201,20 @@ def tile_picked_twohop8_none_p_kernel(
         nc.sync.dma_start(plane(h_all, 1), h_window[1][:, whole])
         add_own(2)
         nc.sync.dma_start(plane(h_all, 2), h_window[2][:, whole])
-        w2_late = round_w2(1, "weighted0")
         fetch_far(1, whole)
         fetch_far(2, whole)
-        fetch_second(3)
-        quantise_w2(0, w2_early)
-        weigh(3)
-        quantise_w2(1, w2_late)
-        add_own(3)
-        nc.vector.tensor_copy(plane(h_all, 3), h_window[3][:, whole])
-        for cols in blocks:
-            fetch_far(3, cols)
+        nc.vector.tensor_tensor(both[3][:], first[3][:], second[:], ADD)
+        nc.vector.tensor_copy(*w2_block(3))
+        for cols in halves:
+            weigh(3, cols)
+        for cols in halves:
+            add_own(3, cols)
+        for u in range(2):
+            quantise_w2(u)
+        for u in range(2):
+            nc.scalar.copy(plane(h_all, 3, halves[u]), h_window[3][:, halves[u]])
+            for cols in blocks[2 * u : 2 * u + 2]:
+                fetch_far(3, cols)
 
         out_rows = out.rearrange("(b p) n -> p b n", p=P)
 

@@ -165,12 +165,12 @@ def tile_picked_twohop8_none_p_kernel(
         def fetch_far(t, cols):
             nc.scalar.activation(plane(far, t, cols), h_window[t][:].indirect(entries(q1_sb, cols)), COPY)
 
-        w2_bf = keep.tile([P, N, PACK], BF16, name="w2_bf", tag="x_table_then_w2_bf", align_bytes=64)
+        w2_bf = [keep.tile([P, N // 2, PACK], BF16, name="w2_bf0", tag="x_table_then_w2_bf", **shared)]
 
         def w2_block(b):
             source = (w2_early, w2_late)[b // 2][:, :, blocks[b % 2]]
             return (
-                w2_bf[:, blocks[b], :].rearrange("p (c i) t -> p c t i", i=4),
+                w2_bf[b // 2][:, blocks[b % 2], :].rearrange("p (c i) t -> p c t i", i=4),
                 source.rearrange("p t (c i) -> p c t i", i=4),
             )
 
@@ -178,10 +178,10 @@ def tile_picked_twohop8_none_p_kernel(
             nc.vector.quantize_mx(
                 w2_codes[:, halves[u]].bitcast(FP8X4),
                 w2_scale[:, halves[u]],
-                w2_bf[:, halves[u], :].rearrange("p n j -> p (n j)"),
+                w2_bf[u][:].rearrange("p n j -> p (n j)"),
             )
 
-        for b in range(3):
+        for b in range(2):
             nc.gpsimd.tensor_scalar(*w2_block(b), 1.0, 0.0, MULT, ADD)
         for t in range(PACK):
             fetch_first(t)
@@ -195,12 +195,15 @@ def tile_picked_twohop8_none_p_kernel(
         add_own(0)
         nc.sync.dma_start(plane(h_all, 0), h_window[0][:, whole])
         fetch_far(0, whole)
+        w2_bf.append(keep.tile([P, N // 2, PACK], BF16, name="w2_bf1", tag="weighted0", **shared))
+        nc.scalar.copy(*w2_block(2))
         weigh(1)
         weigh(2)
         add_own(1)
         nc.sync.dma_start(plane(h_all, 1), h_window[1][:, whole])
-        add_own(2)
-        nc.sync.dma_start(plane(h_all, 2), h_window[2][:, whole])
+        for cols in halves:
+            add_own(2, cols)
+            nc.sync.dma_start(plane(h_all, 2, cols), h_window[2][:, cols])
         fetch_far(1, whole)
         fetch_far(2, whole)
         nc.vector.tensor_tensor(both[3][:], first[3][:], second[:], ADD)
@@ -260,7 +263,7 @@ def tile_picked_twohop8_none_p_kernel(
                 )
 
         z_bf = [difference(0), difference(1)]
-        finish(0, z_bf[0], [7])
+        finish(0, z_bf[0], [4])
         z_bf.append(difference(2))
         finish(1, z_bf[1], [3])
         z_bf.append(difference(3))

@@ -189,27 +189,24 @@ def tile_picked_twohop8_none_p_kernel(
         nc.scalar.activation(second[:], y[3][:].indirect(p2_sb[:]), COPY)
 
         fetch_second(0)
+        w2_bf.append(keep.tile([P, N // 2, PACK], BF16, name="w2_bf1", tag="first0", **shared))
         fetch_second(1)
         weigh(0)
-        fetch_second(2)
-        add_own(0)
-        nc.sync.dma_start(plane(h_all, 0), h_window[0][:, whole])
-        fetch_far(0, whole)
-        w2_bf.append(keep.tile([P, N // 2, PACK], BF16, name="w2_bf1", tag="weighted0", **shared))
-        nc.scalar.copy(*w2_block(2))
         weigh(1)
+        fetch_second(2)
+        for b in range(2, 4):
+            nc.scalar.copy(*w2_block(b))
+        for t in range(2):
+            add_own(t)
+            nc.sync.dma_start(plane(h_all, t), h_window[t][:, whole])
+            fetch_far(t, whole)
         weigh(2)
-        add_own(1)
-        nc.sync.dma_start(plane(h_all, 1), h_window[1][:, whole])
-        for cols in halves:
-            add_own(2, cols)
-            nc.sync.dma_start(plane(h_all, 2, cols), h_window[2][:, cols])
-        fetch_far(1, whole)
-        fetch_far(2, whole)
         nc.vector.tensor_tensor(both[3][:], first[3][:], second[:], ADD)
-        nc.vector.tensor_copy(*w2_block(3))
+        add_own(2)
+        fetch_far(2, whole)
         for cols in halves:
             weigh(3, cols)
+        nc.vector.tensor_copy(plane(h_all, 2), h_window[2][:, whole])
         for cols in halves:
             add_own(3, cols)
         for u in range(2):

@@ -21,6 +21,7 @@ P = 128
 PACK = 4
 LIST_ROWS = 16
 WIDE = 1024
+SCALAR_SHARE = 64
 
 
 def tile_picked_twohop8_none_p_kernel(
@@ -43,19 +44,16 @@ def tile_picked_twohop8_none_p_kernel(
         p2_sb = lists.tile([P, S // LIST_ROWS], U16, name="p2_sb")
         q1_sb = lists.tile([P, S // LIST_ROWS], U16, name="q1_sb")
 
-        w1_raw = [
-            keep.tile([P, PACK, H // 2], F32, name="w1_raw%d" % u, tag=tag)
-            for u, tag in enumerate(("w1_raw0", "w1_raw_then_w2_raw"))
-        ]
+        w1_raw = keep.tile([P, PACK, H], F32, name="w1_raw", tag="w1_raw_then_w2_raw")
         x_table = keep.tile([P, T], I32, name="x_table", tag="x_table_then_w2_bf", align_bytes=64)
         scale_table = keep.tile([P, T], U8, name="scale_table", align_bytes=64)
 
         nc.vector.memset(scale_table[:].bitcast(I32), 0)
         w1_rows = w1.rearrange("(p j) c -> p j c", j=PACK)
-        nc.sync.dma_start(w1_raw[0][:], w1_rows[:, :, : H // 2])
+        nc.sync.dma_start(w1_raw[:, :2, :], w1_rows[:, :2, :])
         nc.sync.dma_start(offs_sb[:], offs)
         nc.sync.dma_start(scale_table[0:P:8, :].bitcast(I32), x_scales[0].bitcast(I32))
-        nc.sync.dma_start(w1_raw[1][:], w1_rows[:, :, H // 2 :])
+        nc.sync.dma_start(w1_raw[:, 2:, :], w1_rows[:, 2:, :])
         nc.sync.dma_start(x_table[:], x_words[0].rearrange("p n t -> p (n t)").bitcast(I32))
         nc.sync.dma_start(p1_sb[:], p1)
         nc.sync.dma_start(p2_sb[:], p2)
@@ -63,9 +61,9 @@ def tile_picked_twohop8_none_p_kernel(
 
         w1_bf = keep.tile([P, PACK * H], BF16, name="w1_bf", tag="w1_bf_then_w2_raw", align_bytes=64)
         w1_dealt = w1_bf[:].rearrange("p (t m j) -> p m j t", t=PACK, j=PACK)
-        nc.scalar.activation(
-            w1_dealt[:, : P // 2], w1_raw[0][:].rearrange("p j (m t) -> p m j t", t=PACK), COPY
-        )
+        w1_source = w1_raw[:].rearrange("p j (m t) -> p m j t", t=PACK)
+        for rows in (slice(0, 2), slice(2, 4)):
+            nc.scalar.activation(w1_dealt[:, :SCALAR_SHARE, rows], w1_source[:, :SCALAR_SHARE, rows], COPY)
 
         picked_scale = keep.tile([P, S], U8, name="picked_scale", tag="picked_then_ga", align_bytes=64)
         nc.vector.tensor_copy(picked_scale[:], scale_table[:].indirect(offs_sb[:]))
@@ -76,9 +74,7 @@ def tile_picked_twohop8_none_p_kernel(
                 x_scale[j:P:32, :].bitcast(I32), picked_scale[8 * j : P : 32, :].bitcast(I32)
             )
 
-        nc.vector.tensor_copy(
-            w1_dealt[:, P // 2 :], w1_raw[1][:].rearrange("p j (m t) -> p m j t", t=PACK)
-        )
+        nc.vector.tensor_copy(w1_dealt[:, SCALAR_SHARE:], w1_source[:, SCALAR_SHARE:])
         w2_rows = w2.rearrange("(p j) c -> p j c", j=PACK)
         w2_early = keep.tile([P, PACK, N // 2], F32, name="w2_early", tag="w1_raw_then_w2_raw")
         nc.sync.dma_start(w2_early[:], w2_rows[:, :, : N // 2])

@@ -248,7 +248,7 @@ def tile_picked_twohop8_none_p_kernel(
                         start=True,
                         stop=True,
                     )
-                copy = nc.vector.tensor_copy if n == 1 else nc.scalar.copy
+                copy = nc.vector.tensor_copy if (b, n) == (3, 1) else nc.scalar.copy
                 copy(result[:, cols], acc[:, cols])
                 nc.sync.dma_start(
                     out_rows[:, cols.start // P : cols.stop // P, blocks[b]],
@@ -256,9 +256,9 @@ def tile_picked_twohop8_none_p_kernel(
                 )
 
         z_bf = [difference(0), difference(1)]
-        finish(0, z_bf[0], [4])
+        finish(0, z_bf[0], [7, 0])
         z_bf.append(difference(2))
-        finish(1, z_bf[1], [3])
+        finish(1, z_bf[1], [1, 2])
         z_bf.append(difference(3))
-        finish(2, z_bf[2], [2])
-        finish(3, z_bf[3], [0, 1])
+        finish(2, z_bf[2], [3, 4])
+        finish(3, z_bf[3], [5, 6])

@@ -227,38 +227,45 @@ def tile_picked_twohop8_none_p_kernel(
             )
             return z_bf
 
-        def finish(b, z_bf, banks):
-            z_codes = keep.tile([P, P], U32, name="z_codes%d" % b, align_bytes=64)
-            z_scale = keep.tile([P, P], U8, name="z_scale%d" % b, align_bytes=64)
-            nc.vector.quantize_mx(
-                z_codes[:].bitcast(FP8X4), z_scale[:], z_bf[:].rearrange("p n t -> p (n t)")
+        def quantise_z(z_bf, codes, scale):
+            nc.vector.quantize_mx(codes.bitcast(FP8X4), scale, z_bf[:].rearrange("p n t -> p (n t)"))
+
+        def z_operand(name, width):
+            return (
+                keep.tile([P, width], U32, name="z_codes" + name, align_bytes=64),
+                keep.tile([P, width], U8, name="z_scale" + name, align_bytes=64),
             )
-            result = keep.tile([P, N], F32, name="result%d" % b)
-            share = N // len(banks)
+
+        def finish(nodes, operand, banks, copies):
+            width = nodes.stop - nodes.start
+            result = keep.tile([P, PACK, width], F32, name="result%d" % nodes.start)
+            share = PACK // len(banks)
             for n, at in enumerate(banks):
                 acc = bank(at)
-                cols = slice(n * share, (n + 1) * share)
-                for rows in blocks[cols.start // P : cols.stop // P]:
+                for m in range(share):
+                    rows = blocks[n * share + m]
                     nc.tensor.matmul_mx(
-                        acc[:, rows],
+                        acc[:, m * width : (m + 1) * width],
                         lhsT=w2_codes[:, rows].bitcast(FP8X4),
                         lhsT_scale=w2_scale[:, rows],
-                        rhs=z_codes[:].bitcast(FP8X4),
-                        rhs_scale=z_scale[:],
+                        rhs=operand[0][:].bitcast(FP8X4),
+                        rhs_scale=operand[1][:],
                         start=True,
                         stop=True,
                     )
-                copy = nc.vector.tensor_copy if (b, n) == (3, 1) else nc.scalar.copy
-                copy(result[:, cols], acc[:, cols])
-                nc.sync.dma_start(
-                    out_rows[:, cols.start // P : cols.stop // P, blocks[b]],
-                    result[:, cols].rearrange("p (b n) -> p b n", n=P),
-                )
+                part = result[:, n * share : (n + 1) * share, :]
+                copies[n](part.rearrange("p m n -> p (m n)"), acc[:, : share * width])
+                nc.sync.dma_start(out_rows[:, n * share : (n + 1) * share, nodes], part)
 
+        narrow = [z_operand("0", P), z_operand("1", P)]
+        wide = z_operand("2", 2 * P)
         z_bf = [difference(0), difference(1)]
-        finish(0, z_bf[0], [7, 0])
+        quantise_z(z_bf[0], narrow[0][0][:], narrow[0][1][:])
+        finish(blocks[0], narrow[0], [7, 0], [nc.scalar.copy] * 2)
         z_bf.append(difference(2))
-        finish(1, z_bf[1], [1, 2])
+        quantise_z(z_bf[1], narrow[1][0][:], narrow[1][1][:])
+        finish(blocks[1], narrow[1], [1, 2], [nc.scalar.copy] * 2)
         z_bf.append(difference(3))
-        finish(2, z_bf[2], [3, 4])
-        finish(3, z_bf[3], [5, 6])
+        for u in range(2):
+            quantise_z(z_bf[2 + u], wide[0][:, blocks[u]], wide[1][:, blocks[u]])
+        finish(halves[1], wide, [3, 4, 5, 6], [nc.scalar.copy, nc.vector.tensor_copy] * 2)

@@ -123,13 +123,17 @@ def tile_picked_twohop8_none_p_kernel(
         make_y(0, x_parts[2], 3, nc.scalar.copy)
         make_y(1, halves[1], 4, nc.vector.tensor_copy)
         make_y(2, whole, 5, nc.vector.tensor_copy)
-        make_y(3, whole, 6, nc.vector.tensor_copy)
+        make_y(3, halves[0], 6, nc.vector.tensor_copy)
+        late_bank = bank(6)
+        first_product(late_bank, 3, halves[1])
 
         shared = dict(align_bytes=64)
         first = [
             keep.tile([P, S], F32, name="first%d" % t, tag="first%d" % t, **shared) for t in range(PACK)
         ]
-        both = [keep.tile([P, S], F32, name="both%d" % t) for t in range(PACK)]
+        both = [
+            keep.tile([P, S], F32, name="both%d" % t, tag="both%d" % t, **shared) for t in range(PACK)
+        ]
         weighted = [
             keep.tile([P, S], F32, name="weighted%d" % t, tag="weighted%d" % t, **shared)
             for t in range(PACK)
@@ -140,7 +144,6 @@ def tile_picked_twohop8_none_p_kernel(
             for t in range(PACK)
         ]
         far = keep.tile([P, PACK * S], F32, name="far")
-        w2_codes = keep.tile([P, N], U32, name="w2_codes", align_bytes=64)
         w2_scale = keep.tile([P, N], U8, name="w2_scale", align_bytes=64)
 
         def plane(tile, t, cols=whole):
@@ -179,8 +182,10 @@ def tile_picked_twohop8_none_p_kernel(
 
         for b in range(2):
             nc.gpsimd.tensor_scalar(*w2_block(b), 1.0, 0.0, MULT, ADD)
-        for t in range(PACK):
+        for t in range(PACK - 1):
             fetch_first(t)
+        nc.scalar.copy(y[3][:, halves[1]], late_bank[:, halves[1]])
+        fetch_first(3)
         second = keep.tile([P, S], F32, name="second")
         nc.scalar.activation(second[:], y[3][:].indirect(p2_sb[:]), COPY)
 
@@ -199,36 +204,37 @@ def tile_picked_twohop8_none_p_kernel(
         weigh(2)
         nc.vector.tensor_tensor(both[3][:], first[3][:], second[:], ADD)
         add_own(2)
-        fetch_far(2, whole)
-        for cols in halves:
-            weigh(3, cols)
+        fetch_far(2, halves[0])
+        staged = [weighted[3][:, halves[0]], plane(far, 2, halves[1])]
+        for u in range(2):
+            nc.vector.tensor_tensor(staged[u], both[3][:, halves[u]], ga_sb[:, halves[u]], MULT)
+        for u in range(2):
+            nc.vector.tensor_tensor(h_window[3][:, halves[u]], staged[u], y[3][:, halves[u]], ADD)
         nc.vector.tensor_copy(plane(h_all, 2), h_window[2][:, whole])
-        for cols in halves:
-            add_own(3, cols)
-        for u in range(2):
-            quantise_w2(u)
-        for u in range(2):
-            nc.scalar.copy(plane(h_all, 3, halves[u]), h_window[3][:, halves[u]])
-            for cols in blocks[2 * u : 2 * u + 2]:
-                fetch_far(3, cols)
+        nc.vector.tensor_copy(plane(h_all, 3, halves[0]), h_window[3][:, halves[0]])
+        w2_codes = keep.tile([P, N], U32, name="w2_codes", tag="both3", **shared)
+        quantise_w2(0)
+        fetch_far(3, blocks[0])
+        fetch_far(3, blocks[1])
+        fetch_far(2, halves[1])
+        nc.scalar.copy(plane(h_all, 3, halves[1]), h_window[3][:, halves[1]])
+        fetch_far(3, blocks[2])
+        fetch_far(3, blocks[3])
 
         out_rows = out.rearrange("(b p) n -> p b n", p=P)
 
         def by_fours(tile, cols):
             return tile[:].rearrange("p (t c i) -> p c t i", t=PACK, i=4)[:, cols.start // 4 : cols.stop // 4]
 
+        z_bf = [keep.tile([P, 2 * P, PACK], BF16, name="z_bf%d" % u, align_bytes=64) for u in range(2)]
+
         def difference(b):
-            z_bf = keep.tile([P, P, PACK], BF16, name="z_bf%d" % b, align_bytes=64)
             nc.vector.tensor_tensor(
-                z_bf[:].rearrange("p (c i) t -> p c t i", i=4),
+                z_bf[b // 2][:, blocks[b % 2], :].rearrange("p (c i) t -> p c t i", i=4),
                 by_fours(h_all, blocks[b]),
                 by_fours(far, blocks[b]),
                 SUBTRACT,
             )
-            return z_bf
-
-        def quantise_z(z_bf, codes, scale):
-            nc.vector.quantize_mx(codes.bitcast(FP8X4), scale, z_bf[:].rearrange("p n t -> p (n t)"))
 
         def z_operand(name, width):
             return (
@@ -236,36 +242,45 @@ def tile_picked_twohop8_none_p_kernel(
                 keep.tile([P, width], U8, name="z_scale" + name, align_bytes=64),
             )
 
-        def finish(nodes, operand, banks, copies):
-            width = nodes.stop - nodes.start
-            result = keep.tile([P, PACK, width], F32, name="result%d" % nodes.start)
-            share = PACK // len(banks)
-            for n, at in enumerate(banks):
-                acc = bank(at)
-                for m in range(share):
-                    rows = blocks[n * share + m]
-                    nc.tensor.matmul_mx(
-                        acc[:, m * width : (m + 1) * width],
-                        lhsT=w2_codes[:, rows].bitcast(FP8X4),
-                        lhsT_scale=w2_scale[:, rows],
-                        rhs=operand[0][:].bitcast(FP8X4),
-                        rhs_scale=operand[1][:],
-                        start=True,
-                        stop=True,
-                    )
-                part = result[:, n * share : (n + 1) * share, :]
-                copies[n](part.rearrange("p m n -> p (m n)"), acc[:, : share * width])
-                nc.sync.dma_start(out_rows[:, n * share : (n + 1) * share, nodes], part)
+        def second_product(u, m, cols, at, copy, result):
+            codes, scale = operands[u]
+            acc = bank(at)
+            nc.tensor.matmul_mx(
+                acc[:, cols],
+                lhsT=w2_codes[:, blocks[m]].bitcast(FP8X4),
+                lhsT_scale=w2_scale[:, blocks[m]],
+                rhs=codes[:, cols].bitcast(FP8X4),
+                rhs_scale=scale[:, cols],
+                start=True,
+                stop=True,
+            )
+            copy(result[:, cols], acc[:, cols])
 
-        narrow = [z_operand("0", P), z_operand("1", P)]
-        wide = z_operand("2", 2 * P)
-        z_bf = [difference(0), difference(1)]
-        quantise_z(z_bf[0], narrow[0][0][:], narrow[0][1][:])
-        finish(blocks[0], narrow[0], [7, 0], [nc.scalar.copy] * 2)
-        z_bf.append(difference(2))
-        quantise_z(z_bf[1], narrow[1][0][:], narrow[1][1][:])
-        finish(blocks[1], narrow[1], [1, 2], [nc.scalar.copy] * 2)
-        z_bf.append(difference(3))
-        for u in range(2):
-            quantise_z(z_bf[2 + u], wide[0][:, blocks[u]], wide[1][:, blocks[u]])
-        finish(halves[1], wide, [3, 4, 5, 6], [nc.scalar.copy, nc.vector.tensor_copy] * 2)
+        def finish(u, m, pieces, copy):
+            result = keep.tile([P, S // 2], F32, name="result%d_%d" % (u, m))
+            for cols, at in pieces:
+                second_product(u, m, cols, at, copy, result)
+            nc.sync.dma_start(out_rows[:, m, halves[u]], result[:])
+
+        operands = [z_operand("%d" % u, 2 * P) for u in range(2)]
+
+        def quantise_z(u, cols):
+            codes, scale = operands[u]
+            nc.vector.quantize_mx(
+                codes[:, cols].bitcast(FP8X4), scale[:, cols], z_bf[u][:, cols, :].rearrange("p n t -> p (n t)")
+            )
+
+        difference(0)
+        difference(1)
+        quantise_w2(1)
+        quantise_z(0, halves[0])
+        for m, at in enumerate((7, 0, 1, 2)):
+            finish(0, m, [(halves[0], at)], nc.scalar.copy)
+        difference(2)
+        difference(3)
+        quantise_z(1, blocks[0])
+        quantise_z(1, blocks[1])
+        finish(1, 0, [(blocks[0], 7), (blocks[1], 3)], nc.scalar.copy)
+        finish(1, 1, [(halves[0], 4)], nc.vector.tensor_copy)
+        finish(1, 2, [(halves[0], 5)], nc.scalar.copy)
+        finish(1, 3, [(halves[0], 6)], nc.vector.tensor_copy)

@@ -213,7 +213,8 @@ def tile_picked_twohop8_none_p_kernel(
         nc.vector.tensor_copy(plane(h_all, 2), h_window[2][:, whole])
         nc.vector.tensor_copy(plane(h_all, 3, halves[0]), h_window[3][:, halves[0]])
         w2_codes = keep.tile([P, N], U32, name="w2_codes", tag="both3", **shared)
-        quantise_w2(0)
+        for u in range(2):
+            quantise_w2(u)
         fetch_far(3, blocks[0])
         fetch_far(3, blocks[1])
         fetch_far(2, halves[1])
@@ -226,61 +227,69 @@ def tile_picked_twohop8_none_p_kernel(
         def by_fours(tile, cols):
             return tile[:].rearrange("p (t c i) -> p c t i", t=PACK, i=4)[:, cols.start // 4 : cols.stop // 4]
 
-        z_bf = [keep.tile([P, 2 * P, PACK], BF16, name="z_bf%d" % u, align_bytes=64) for u in range(2)]
+        z_bf = [keep.tile([P, P, PACK], BF16, name="z_bf%d" % b, align_bytes=64) for b in range(PACK)]
+        groups = [blocks[0], blocks[1], halves[1]]
+        z_codes = [
+            keep.tile([P, g.stop - g.start], U32, name="z_codes%d" % g.start, align_bytes=64) for g in groups
+        ]
+        z_scale = [
+            keep.tile([P, g.stop - g.start], U8, name="z_scale%d" % g.start, align_bytes=64) for g in groups
+        ]
 
         def difference(b):
             nc.vector.tensor_tensor(
-                z_bf[b // 2][:, blocks[b % 2], :].rearrange("p (c i) t -> p c t i", i=4),
+                z_bf[b][:].rearrange("p (c i) t -> p c t i", i=4),
                 by_fours(h_all, blocks[b]),
                 by_fours(far, blocks[b]),
                 SUBTRACT,
             )
 
-        def z_operand(name, width):
-            return (
-                keep.tile([P, width], U32, name="z_codes" + name, align_bytes=64),
-                keep.tile([P, width], U8, name="z_scale" + name, align_bytes=64),
+        def quantise_z(b, g, cols):
+            nc.vector.quantize_mx(
+                z_codes[g][:, cols].bitcast(FP8X4),
+                z_scale[g][:, cols],
+                z_bf[b][:].rearrange("p n t -> p (n t)"),
             )
 
-        def second_product(u, m, cols, at, copy, result):
-            codes, scale = operands[u]
-            acc = bank(at)
+        def second_product(acc, g, m, cols):
             nc.tensor.matmul_mx(
-                acc[:, cols],
+                acc,
                 lhsT=w2_codes[:, blocks[m]].bitcast(FP8X4),
                 lhsT_scale=w2_scale[:, blocks[m]],
-                rhs=codes[:, cols].bitcast(FP8X4),
-                rhs_scale=scale[:, cols],
+                rhs=z_codes[g][:, cols].bitcast(FP8X4),
+                rhs_scale=z_scale[g][:, cols],
                 start=True,
                 stop=True,
             )
-            copy(result[:, cols], acc[:, cols])
 
-        def finish(u, m, pieces, copy):
-            result = keep.tile([P, S // 2], F32, name="result%d_%d" % (u, m))
+        def finish_narrow(g, banks):
+            for u, at in enumerate(banks):
+                acc = bank(at)
+                for n in range(2):
+                    second_product(acc[:, blocks[n]], g, 2 * u + n, blocks[0])
+                result = keep.tile([P, 2, P], F32, name="narrow%d_%d" % (g, u))
+                nc.scalar.copy(result[:].rearrange("p m n -> p (m n)"), acc[:, halves[0]])
+                nc.sync.dma_start(out_rows[:, 2 * u : 2 * u + 2, groups[g]], result[:])
+
+        def finish_wide(m, pieces, copy):
+            result = keep.tile([P, 2 * P], F32, name="wide%d" % m)
             for cols, at in pieces:
-                second_product(u, m, cols, at, copy, result)
-            nc.sync.dma_start(out_rows[:, m, halves[u]], result[:])
-
-        operands = [z_operand("%d" % u, 2 * P) for u in range(2)]
-
-        def quantise_z(u, cols):
-            codes, scale = operands[u]
-            nc.vector.quantize_mx(
-                codes[:, cols].bitcast(FP8X4), scale[:, cols], z_bf[u][:, cols, :].rearrange("p n t -> p (n t)")
-            )
+                acc = bank(at)
+                second_product(acc[:, cols], 2, m, cols)
+                copy(result[:, cols], acc[:, cols])
+            nc.sync.dma_start(out_rows[:, m, groups[2]], result[:])
 
         difference(0)
         difference(1)
-        quantise_w2(1)
-        quantise_z(0, halves[0])
-        for m, at in enumerate((7, 0, 1, 2)):
-            finish(0, m, [(halves[0], at)], nc.scalar.copy)
+        quantise_z(0, 0, blocks[0])
+        finish_narrow(0, (7, 0))
         difference(2)
+        quantise_z(1, 1, blocks[0])
+        finish_narrow(1, (1, 2))
         difference(3)
-        quantise_z(1, blocks[0])
-        quantise_z(1, blocks[1])
-        finish(1, 0, [(blocks[0], 7), (blocks[1], 3)], nc.scalar.copy)
-        finish(1, 1, [(halves[0], 4)], nc.vector.tensor_copy)
-        finish(1, 2, [(halves[0], 5)], nc.scalar.copy)
-        finish(1, 3, [(halves[0], 6)], nc.vector.tensor_copy)
+        quantise_z(2, 2, blocks[0])
+        quantise_z(3, 2, blocks[1])
+        finish_wide(0, [(blocks[0], 7), (blocks[1], 3)], nc.scalar.copy)
+        finish_wide(1, [(halves[0], 4)], nc.vector.tensor_copy)
+        finish_wide(2, [(halves[0], 5)], nc.scalar.copy)
+        finish_wide(3, [(halves[0], 6)], nc.vector.tensor_copy)

@@ -1,6 +1,7 @@
 from contextlib import ExitStack
 
 import concourse.mybir as mybir
+from concourse.masks import make_identity
 
 K, T, S, N, H = 512, 2048, 512, 512, 512
 FLOPS = 2 * K * H * S + 2 * H * N * S
@@ -85,8 +86,11 @@ def tile_picked_twohop8_none_p_kernel(
             [P, PACK, N // 2], F32, name="w2_late", tag="w1_bf_then_w2_raw", align_bytes=64
         )
         nc.sync.dma_start(w2_late[:], w2_rows[:, :, N // 2 :])
-        ga_sb = keep.tile([P, S], F32, name="ga_sb", tag="picked_then_ga", align_bytes=64)
-        nc.sync.dma_start(ga_sb[:], ga)
+        ga_column = keep.tile([P, S // P], F32, name="ga_column", tag="picked_then_ga", align_bytes=64)
+        with nc.allow_non_contiguous_dma(reason="one weight a partition"):
+            nc.sync.dma_start(ga_column[:], ga[0].rearrange("(b p) -> p b", p=P))
+        identity = keep.tile([P, P], F32, name="identity")
+        make_identity(nc, identity[:])
 
         x_codes = keep.tile([P, S], U32, name="x_codes", align_bytes=64)
         halves = [slice(0, S // 2), slice(S // 2, S)]
@@ -112,10 +116,13 @@ def tile_picked_twohop8_none_p_kernel(
 
         y = [keep.tile([P, WIDE], F32, name="y%d" % t) for t in range(PACK)]
 
+        y_banks = [[] for t in range(PACK)]
+
         def make_y(t, cols, at, copy):
             acc = bank(at)
             first_product(acc, t, cols)
             copy(y[t][:, cols], acc[:, cols])
+            y_banks[t].append((cols, acc))
 
         make_y(0, x_parts[0], 0, nc.scalar.copy)
         make_y(1, halves[0], 1, nc.vector.tensor_copy)
@@ -124,8 +131,19 @@ def tile_picked_twohop8_none_p_kernel(
         make_y(1, halves[1], 4, nc.vector.tensor_copy)
         make_y(2, whole, 5, nc.vector.tensor_copy)
         make_y(3, halves[0], 6, nc.vector.tensor_copy)
-        late_bank = bank(6)
+        late_bank = y_banks[3][0][1]
         first_product(late_bank, 3, halves[1])
+        y_banks[3].append((halves[1], late_bank))
+        ga_bank = bank(7)
+        for b, cols in enumerate(blocks):
+            nc.tensor.matmul(
+                ga_bank[:, cols],
+                lhsT=ga_column[:, b : b + 1].to_broadcast([P, P]),
+                rhs=identity[:],
+                is_transpose=True,
+                start=True,
+                stop=True,
+            )
 
         shared = dict(align_bytes=64)
         first = [
@@ -156,10 +174,11 @@ def tile_picked_twohop8_none_p_kernel(
             nc.vector.tensor_tensor(both[t][:], y[t][:].indirect(p2_sb[:]), first[t][:], ADD)
 
         def weigh(t, cols=whole):
-            nc.vector.tensor_tensor(weighted[t][:, cols], both[t][:, cols], ga_sb[:, cols], MULT)
+            nc.vector.tensor_tensor(weighted[t][:, cols], both[t][:, cols], ga_bank[:, cols], MULT)
 
-        def add_own(t, cols=whole):
-            nc.vector.tensor_tensor(h_window[t][:, cols], weighted[t][:, cols], y[t][:, cols], ADD)
+        def add_own(t, term):
+            for cols, acc in y_banks[t]:
+                nc.vector.tensor_tensor(h_window[t][:, cols], term[:, cols], acc[:, cols], ADD)
 
         def fetch_far(t, cols):
             nc.scalar.activation(plane(far, t, cols), h_window[t][:].indirect(entries(q1_sb, cols)), COPY)
@@ -184,33 +203,33 @@ def tile_picked_twohop8_none_p_kernel(
             nc.gpsimd.tensor_scalar(*w2_block(b), 1.0, 0.0, MULT, ADD)
         for t in range(PACK - 1):
             fetch_first(t)
+        second = keep.tile([P, S], F32, name="second")
+        nc.scalar.activation(second[:], y[2][:].indirect(p2_sb[:]), COPY)
         nc.scalar.copy(y[3][:, halves[1]], late_bank[:, halves[1]])
         fetch_first(3)
-        second = keep.tile([P, S], F32, name="second")
-        nc.scalar.activation(second[:], y[3][:].indirect(p2_sb[:]), COPY)
 
         fetch_second(0)
-        w2_bf.append(keep.tile([P, N // 2, PACK], BF16, name="w2_bf1", tag="first0", **shared))
         fetch_second(1)
+        nc.gpsimd.tensor_tensor(both[2][:], first[2][:], second[:], ADD)
         weigh(0)
         weigh(1)
-        fetch_second(2)
-        for b in range(2, 4):
-            nc.scalar.copy(*w2_block(b))
         for t in range(2):
-            add_own(t)
+            add_own(t, weighted[t])
             nc.sync.dma_start(plane(h_all, t), h_window[t][:, whole])
             fetch_far(t, whole)
         weigh(2)
-        nc.vector.tensor_tensor(both[3][:], first[3][:], second[:], ADD)
-        add_own(2)
-        fetch_far(2, halves[0])
+        fetch_second(3)
+        w2_bf.append(keep.tile([P, N // 2, PACK], BF16, name="w2_bf1", tag="first3", **shared))
+        nc.gpsimd.tensor_scalar(*w2_block(2), 1.0, 0.0, MULT, ADD)
+        nc.scalar.copy(*w2_block(3))
         staged = [weighted[3][:, halves[0]], plane(far, 2, halves[1])]
+        add_own(2, weighted[2])
+        nc.gpsimd.tensor_scalar(plane(h_all, 2), h_window[2][:, whole], 1.0, 0.0, MULT, ADD)
+        fetch_far(2, halves[0])
         for u in range(2):
-            nc.vector.tensor_tensor(staged[u], both[3][:, halves[u]], ga_sb[:, halves[u]], MULT)
-        for u in range(2):
-            nc.vector.tensor_tensor(h_window[3][:, halves[u]], staged[u], y[3][:, halves[u]], ADD)
-        nc.vector.tensor_copy(plane(h_all, 2), h_window[2][:, whole])
+            nc.vector.tensor_tensor(staged[u], both[3][:, halves[u]], ga_bank[:, halves[u]], MULT)
+        for u, (cols, acc) in enumerate(y_banks[3]):
+            nc.vector.tensor_tensor(h_window[3][:, cols], staged[u], acc[:, cols], ADD)
         nc.vector.tensor_copy(plane(h_all, 3, halves[0]), h_window[3][:, halves[0]])
         w2_codes = keep.tile([P, N], U32, name="w2_codes", tag="both3", **shared)
         for u in range(2):
@@ -289,7 +308,7 @@ def tile_picked_twohop8_none_p_kernel(
         difference(3)
         quantise_z(2, 2, blocks[0])
         quantise_z(3, 2, blocks[1])
-        finish_wide(0, [(blocks[0], 7), (blocks[1], 3)], nc.scalar.copy)
+        finish_wide(0, [(blocks[0], 7), (blocks[1], 3)], nc.vector.tensor_copy)
         finish_wide(1, [(halves[0], 4)], nc.vector.tensor_copy)
         finish_wide(2, [(halves[0], 5)], nc.scalar.copy)
         finish_wide(3, [(halves[0], 6)], nc.vector.tensor_copy)

@@ -203,25 +203,25 @@ def tile_picked_twohop8_none_p_kernel(
             nc.gpsimd.tensor_scalar(*w2_block(b), 1.0, 0.0, MULT, ADD)
         for t in range(PACK - 1):
             fetch_first(t)
-        second = keep.tile([P, S], F32, name="second")
-        nc.scalar.activation(second[:], y[2][:].indirect(p2_sb[:]), COPY)
         nc.scalar.copy(y[3][:, halves[1]], late_bank[:, halves[1]])
         fetch_first(3)
+        second = keep.tile([P, S], F32, name="second")
+        nc.scalar.activation(second[:], y[3][:].indirect(p2_sb[:]), COPY)
 
         fetch_second(0)
         fetch_second(1)
-        nc.gpsimd.tensor_tensor(both[2][:], first[2][:], second[:], ADD)
         weigh(0)
         weigh(1)
+        fetch_second(2)
+        w2_bf.append(keep.tile([P, N // 2, PACK], BF16, name="w2_bf1", tag="first2", **shared))
+        nc.gpsimd.tensor_scalar(*w2_block(2), 1.0, 0.0, MULT, ADD)
+        nc.gpsimd.tensor_tensor(both[3][:], first[3][:], second[:], ADD)
+        nc.scalar.copy(*w2_block(3))
         for t in range(2):
             add_own(t, weighted[t])
             nc.sync.dma_start(plane(h_all, t), h_window[t][:, whole])
             fetch_far(t, whole)
         weigh(2)
-        fetch_second(3)
-        w2_bf.append(keep.tile([P, N // 2, PACK], BF16, name="w2_bf1", tag="first3", **shared))
-        nc.gpsimd.tensor_scalar(*w2_block(2), 1.0, 0.0, MULT, ADD)
-        nc.scalar.copy(*w2_block(3))
         staged = [weighted[3][:, halves[0]], plane(far, 2, halves[1])]
         add_own(2, weighted[2])
         nc.gpsimd.tensor_scalar(plane(h_all, 2), h_window[2][:, whole], 1.0, 0.0, MULT, ADD)

@@ -149,9 +149,7 @@ def tile_picked_twohop8_none_p_kernel(
         first = [
             keep.tile([P, S], F32, name="first%d" % t, tag="first%d" % t, **shared) for t in range(PACK)
         ]
-        both = [
-            keep.tile([P, S], F32, name="both%d" % t, tag="both%d" % t, **shared) for t in range(PACK)
-        ]
+        both = [keep.tile([P, S], F32, name="both%d" % t) for t in range(PACK - 1)]
         weighted = [
             keep.tile([P, S], F32, name="weighted%d" % t, tag="weighted%d" % t, **shared)
             for t in range(PACK)
@@ -208,30 +206,35 @@ def tile_picked_twohop8_none_p_kernel(
         second = keep.tile([P, S], F32, name="second")
         nc.scalar.activation(second[:], y[3][:].indirect(p2_sb[:]), COPY)
 
-        fetch_second(0)
-        fetch_second(1)
-        weigh(0)
-        weigh(1)
-        fetch_second(2)
-        w2_bf.append(keep.tile([P, N // 2, PACK], BF16, name="w2_bf1", tag="first2", **shared))
-        nc.gpsimd.tensor_scalar(*w2_block(2), 1.0, 0.0, MULT, ADD)
-        nc.gpsimd.tensor_tensor(both[3][:], first[3][:], second[:], ADD)
-        nc.scalar.copy(*w2_block(3))
-        for t in range(2):
+        def finish_plane(t):
             add_own(t, weighted[t])
             nc.sync.dma_start(plane(h_all, t), h_window[t][:, whole])
             fetch_far(t, whole)
+
+        fetch_second(0)
+        fetch_second(1)
+        w2_bf.append(keep.tile([P, N // 2, PACK], BF16, name="w2_bf1", tag="first1", **shared))
+        nc.gpsimd.tensor_scalar(*w2_block(2), 1.0, 0.0, MULT, ADD)
+        nc.scalar.copy(*w2_block(3))
+        weigh(0)
+        weigh(1)
+        finish_plane(0)
+        fetch_second(2)
+        both.append(keep.tile([P, S], F32, name="both3", tag="first2", **shared))
+        for cols in halves:
+            nc.gpsimd.tensor_tensor(both[3][:, cols], first[3][:, cols], second[:, cols], ADD)
+        finish_plane(1)
         weigh(2)
         staged = [weighted[3][:, halves[0]], plane(far, 2, halves[1])]
+        nc.vector.tensor_tensor(staged[0], both[3][:, halves[0]], ga_bank[:, halves[0]], MULT)
         add_own(2, weighted[2])
         nc.gpsimd.tensor_scalar(plane(h_all, 2), h_window[2][:, whole], 1.0, 0.0, MULT, ADD)
         fetch_far(2, halves[0])
-        for u in range(2):
-            nc.vector.tensor_tensor(staged[u], both[3][:, halves[u]], ga_bank[:, halves[u]], MULT)
+        nc.vector.tensor_tensor(staged[1], both[3][:, halves[1]], ga_bank[:, halves[1]], MULT)
         for u, (cols, acc) in enumerate(y_banks[3]):
             nc.vector.tensor_tensor(h_window[3][:, cols], staged[u], acc[:, cols], ADD)
         nc.vector.tensor_copy(plane(h_all, 3, halves[0]), h_window[3][:, halves[0]])
-        w2_codes = keep.tile([P, N], U32, name="w2_codes", tag="both3", **shared)
+        w2_codes = keep.tile([P, N], U32, name="w2_codes", tag="first2", **shared)
         for u in range(2):
             quantise_w2(u)
         fetch_far(3, blocks[0])

@@ -23,6 +23,7 @@ PACK = 4
 LIST_ROWS = 16
 WIDE = 1024
 SCALAR_SHARE = 64
+UNDER_WEIGHINGS = 192
 
 
 def tile_picked_twohop8_none_p_kernel(
@@ -174,8 +175,8 @@ def tile_picked_twohop8_none_p_kernel(
         def weigh(t, cols=whole):
             nc.vector.tensor_tensor(weighted[t][:, cols], both[t][:, cols], ga_bank[:, cols], MULT)
 
-        def add_own(t, term):
-            for cols, acc in y_banks[t]:
+        def add_own(t, term, pieces=slice(None)):
+            for cols, acc in y_banks[t][pieces]:
                 nc.vector.tensor_tensor(h_window[t][:, cols], term[:, cols], acc[:, cols], ADD)
 
         def fetch_far(t, cols):
@@ -183,12 +184,14 @@ def tile_picked_twohop8_none_p_kernel(
 
         w2_bf = [keep.tile([P, N // 2, PACK], BF16, name="w2_bf0", tag="x_table_then_w2_bf", **shared)]
 
-        def w2_block(b):
-            source = (w2_early, w2_late)[b // 2][:, :, blocks[b % 2]]
+        def w2_part(u, cols):
             return (
-                w2_bf[b // 2][:, blocks[b % 2], :].rearrange("p (c i) t -> p c t i", i=4),
-                source.rearrange("p t (c i) -> p c t i", i=4),
+                w2_bf[u][:, cols, :].rearrange("p (c i) t -> p c t i", i=4),
+                (w2_early, w2_late)[u][:, :, cols].rearrange("p t (c i) -> p c t i", i=4),
             )
+
+        def round_w2(u, cols):
+            nc.gpsimd.tensor_scalar(*w2_part(u, cols), 1.0, 0.0, MULT, ADD)
 
         def quantise_w2(u):
             nc.vector.quantize_mx(
@@ -197,8 +200,8 @@ def tile_picked_twohop8_none_p_kernel(
                 w2_bf[u][:].rearrange("p n j -> p (n j)"),
             )
 
-        for b in range(2):
-            nc.gpsimd.tensor_scalar(*w2_block(b), 1.0, 0.0, MULT, ADD)
+        for cols in blocks[:2]:
+            round_w2(0, cols)
         for t in range(PACK - 1):
             fetch_first(t)
         nc.scalar.copy(y[3][:, halves[1]], late_bank[:, halves[1]])
@@ -206,24 +209,25 @@ def tile_picked_twohop8_none_p_kernel(
         second = keep.tile([P, S], F32, name="second")
         nc.scalar.activation(second[:], y[3][:].indirect(p2_sb[:]), COPY)
 
-        def finish_plane(t):
-            add_own(t, weighted[t])
+        def finish_plane(t, pieces=slice(None)):
+            add_own(t, weighted[t], pieces)
             nc.sync.dma_start(plane(h_all, t), h_window[t][:, whole])
             fetch_far(t, whole)
 
         fetch_second(0)
         fetch_second(1)
         w2_bf.append(keep.tile([P, N // 2, PACK], BF16, name="w2_bf1", tag="first1", **shared))
-        nc.gpsimd.tensor_scalar(*w2_block(2), 1.0, 0.0, MULT, ADD)
-        nc.scalar.copy(*w2_block(3))
+        round_w2(1, slice(0, UNDER_WEIGHINGS))
+        nc.scalar.copy(*w2_part(1, slice(UNDER_WEIGHINGS, N // 2)))
         weigh(0)
         weigh(1)
         finish_plane(0)
+        add_own(1, weighted[1], slice(0, 1))
         fetch_second(2)
         both.append(keep.tile([P, S], F32, name="both3", tag="first2", **shared))
         for cols in halves:
             nc.gpsimd.tensor_tensor(both[3][:, cols], first[3][:, cols], second[:, cols], ADD)
-        finish_plane(1)
+        finish_plane(1, slice(1, 2))
         weigh(2)
         staged = [weighted[3][:, halves[0]], plane(far, 2, halves[1])]
         nc.vector.tensor_tensor(staged[0], both[3][:, halves[0]], ga_bank[:, halves[0]], MULT)
@@ -235,8 +239,7 @@ def tile_picked_twohop8_none_p_kernel(
             nc.vector.tensor_tensor(h_window[3][:, cols], staged[u], acc[:, cols], ADD)
         nc.vector.tensor_copy(plane(h_all, 3, halves[0]), h_window[3][:, halves[0]])
         w2_codes = keep.tile([P, N], U32, name="w2_codes", tag="first2", **shared)
-        for u in range(2):
-            quantise_w2(u)
+        quantise_w2(0)
         fetch_far(3, blocks[0])
         fetch_far(3, blocks[1])
         fetch_far(2, halves[1])
@@ -302,9 +305,10 @@ def tile_picked_twohop8_none_p_kernel(
             nc.sync.dma_start(out_rows[:, m, groups[2]], result[:])
 
         difference(0)
-        difference(1)
+        quantise_w2(1)
         quantise_z(0, 0, blocks[0])
         finish_narrow(0, (7, 0))
+        difference(1)
         difference(2)
         quantise_z(1, 1, blocks[0])
         finish_narrow(1, (1, 2))

@@ -131,10 +131,9 @@ def tile_picked_twohop8_none_p_kernel(
         make_y(0, x_parts[2], 3, nc.scalar.copy)
         make_y(1, halves[1], 4, nc.vector.tensor_copy)
         make_y(2, whole, 5, nc.vector.tensor_copy)
-        make_y(3, halves[0], 6, nc.vector.tensor_copy)
-        late_bank = y_banks[3][0][1]
-        first_product(late_bank, 3, halves[1])
-        y_banks[3].append((halves[1], late_bank))
+        late_bank = bank(6)
+        first_product(late_bank, 3, whole)
+        y_banks[3] = [(cols, late_bank) for cols in halves]
         ga_bank = bank(7)
         for b, cols in enumerate(blocks):
             nc.tensor.matmul(
@@ -153,7 +152,7 @@ def tile_picked_twohop8_none_p_kernel(
         both = [keep.tile([P, S], F32, name="both%d" % t) for t in range(PACK - 1)]
         weighted = [
             keep.tile([P, S], F32, name="weighted%d" % t, tag="weighted%d" % t, **shared)
-            for t in range(PACK)
+            for t in range(PACK - 1)
         ]
         h_all = keep.tile([P, PACK * S], F32, name="h_all")
         h_window = [
@@ -197,14 +196,13 @@ def tile_picked_twohop8_none_p_kernel(
             nc.vector.quantize_mx(
                 w2_codes[:, halves[u]].bitcast(FP8X4),
                 w2_scale[:, halves[u]],
-                w2_bf[u][:].rearrange("p n j -> p (n j)"),
+                w2_bf[u][:, halves[0], :].rearrange("p n j -> p (n j)"),
             )
 
-        for cols in blocks[:2]:
-            round_w2(0, cols)
+        round_w2(0, halves[0])
         for t in range(PACK - 1):
             fetch_first(t)
-        nc.scalar.copy(y[3][:, halves[1]], late_bank[:, halves[1]])
+        nc.scalar.copy(y[3][:, whole], late_bank[:])
         fetch_first(3)
         second = keep.tile([P, S], F32, name="second")
         nc.scalar.activation(second[:], y[3][:].indirect(p2_sb[:]), COPY)
@@ -216,9 +214,8 @@ def tile_picked_twohop8_none_p_kernel(
 
         fetch_second(0)
         fetch_second(1)
-        w2_bf.append(keep.tile([P, N // 2, PACK], BF16, name="w2_bf1", tag="first1", **shared))
+        w2_bf.append(keep.tile([P, UNDER_WEIGHINGS + P, PACK], BF16, name="w2_bf1", tag="first1", **shared))
         round_w2(1, slice(0, UNDER_WEIGHINGS))
-        nc.scalar.copy(*w2_part(1, slice(UNDER_WEIGHINGS, N // 2)))
         weigh(0)
         weigh(1)
         finish_plane(0)
@@ -229,7 +226,8 @@ def tile_picked_twohop8_none_p_kernel(
             nc.gpsimd.tensor_tensor(both[3][:, cols], first[3][:, cols], second[:, cols], ADD)
         finish_plane(1, slice(1, 2))
         weigh(2)
-        staged = [weighted[3][:, halves[0]], plane(far, 2, halves[1])]
+        behind_rounded = w2_bf[1][:, UNDER_WEIGHINGS:, :].rearrange("p n j -> p (n j)").bitcast(F32)
+        staged = [behind_rounded, plane(far, 2, halves[1])]
         nc.vector.tensor_tensor(staged[0], both[3][:, halves[0]], ga_bank[:, halves[0]], MULT)
         add_own(2, weighted[2])
         nc.gpsimd.tensor_scalar(plane(h_all, 2), h_window[2][:, whole], 1.0, 0.0, MULT, ADD)
@@ -238,8 +236,10 @@ def tile_picked_twohop8_none_p_kernel(
         for u, (cols, acc) in enumerate(y_banks[3]):
             nc.vector.tensor_tensor(h_window[3][:, cols], staged[u], acc[:, cols], ADD)
         nc.vector.tensor_copy(plane(h_all, 3, halves[0]), h_window[3][:, halves[0]])
+        nc.vector.tensor_copy(*w2_part(1, slice(UNDER_WEIGHINGS, N // 2)))
         w2_codes = keep.tile([P, N], U32, name="w2_codes", tag="first2", **shared)
-        quantise_w2(0)
+        for u in range(2):
+            quantise_w2(u)
         fetch_far(3, blocks[0])
         fetch_far(3, blocks[1])
         fetch_far(2, halves[1])
@@ -305,10 +305,9 @@ def tile_picked_twohop8_none_p_kernel(
             nc.sync.dma_start(out_rows[:, m, groups[2]], result[:])
 
         difference(0)
-        quantise_w2(1)
+        difference(1)
         quantise_z(0, 0, blocks[0])
         finish_narrow(0, (7, 0))
-        difference(1)
         difference(2)
         quantise_z(1, 1, blocks[0])
         finish_narrow(1, (1, 2))

from contextlib import ExitStack

import concourse.mybir as mybir
from concourse.masks import make_identity

K, T, S, N, H = 512, 2048, 512, 512, 512
FLOPS = 2 * K * H * S + 2 * H * N * S

F32 = mybir.dt.float32
BF16 = mybir.dt.bfloat16
I32 = mybir.dt.int32
U32 = mybir.dt.uint32
U16 = mybir.dt.uint16
U8 = mybir.dt.uint8
FP8X4 = mybir.dt.float8_e4m3fn_x4
MULT = mybir.AluOpType.mult
SUBTRACT = mybir.AluOpType.subtract
ADD = mybir.AluOpType.add
COPY = mybir.ActivationFunctionType.Copy

P = 128
PACK = 4
LIST_ROWS = 16
WIDE = 1024
SCALAR_SHARE = 64
UNDER_WEIGHINGS = 192


def tile_picked_twohop8_none_p_kernel(
    tc, x_words, x_scales, w1, ga, w2, offs, p1, p2, q1, out
):
    nc = tc.nc
    with ExitStack() as ctx:
        lists = ctx.enter_context(tc.tile_pool(name="lists", bufs=1))
        keep = ctx.enter_context(tc.tile_pool(name="keep", bufs=1))
        psum = ctx.enter_context(tc.psum_pool(name="psum", bufs=1))

        def bank(b):
            return psum.tile([P, S], F32, name="bank%d" % b)

        def entries(list_tile, cols):
            return list_tile[:, cols.start // LIST_ROWS : cols.stop // LIST_ROWS]

        offs_sb = lists.tile([P, S // LIST_ROWS], U16, name="offs_sb")
        p1_sb = lists.tile([P, S // LIST_ROWS], U16, name="p1_sb")
        p2_sb = lists.tile([P, S // LIST_ROWS], U16, name="p2_sb")
        q1_sb = lists.tile([P, S // LIST_ROWS], U16, name="q1_sb")

        w1_raw = keep.tile([P, PACK, H], F32, name="w1_raw", tag="w1_raw_then_w2_raw")
        x_table = keep.tile([P, T], I32, name="x_table", tag="x_table_then_w2_bf", align_bytes=64)
        scale_table = keep.tile([P, T], U8, name="scale_table", align_bytes=64)

        nc.vector.memset(scale_table[:].bitcast(I32), 0)
        w1_rows = w1.rearrange("(p j) c -> p j c", j=PACK)
        nc.sync.dma_start(w1_raw[:, :2, :], w1_rows[:, :2, :])
        nc.sync.dma_start(offs_sb[:], offs)
        nc.sync.dma_start(scale_table[0:P:8, :].bitcast(I32), x_scales[0].bitcast(I32))
        nc.sync.dma_start(w1_raw[:, 2:, :], w1_rows[:, 2:, :])
        nc.sync.dma_start(x_table[:], x_words[0].rearrange("p n t -> p (n t)").bitcast(I32))
        nc.sync.dma_start(p1_sb[:], p1)
        nc.sync.dma_start(p2_sb[:], p2)
        nc.sync.dma_start(q1_sb[:], q1)

        w1_bf = keep.tile([P, PACK * H], BF16, name="w1_bf", tag="w1_bf_then_w2_raw", align_bytes=64)
        w1_dealt = w1_bf[:].rearrange("p (t m j) -> p m j t", t=PACK, j=PACK)
        w1_source = w1_raw[:].rearrange("p j (m t) -> p m j t", t=PACK)
        for rows in (slice(0, 2), slice(2, 4)):
            nc.scalar.activation(w1_dealt[:, :SCALAR_SHARE, rows], w1_source[:, :SCALAR_SHARE, rows], COPY)

        picked_scale = keep.tile([P, S], U8, name="picked_scale", tag="picked_then_ga", align_bytes=64)
        nc.vector.tensor_copy(picked_scale[:], scale_table[:].indirect(offs_sb[:]))
        x_scale = keep.tile([P, S], U8, name="x_scale", align_bytes=64)
        nc.vector.tensor_copy(x_scale[:].bitcast(I32), picked_scale[:].bitcast(I32))
        for j in range(1, PACK):
            nc.sync.dma_start(
                x_scale[j:P:32, :].bitcast(I32), picked_scale[8 * j : P : 32, :].bitcast(I32)
            )

        nc.vector.tensor_copy(w1_dealt[:, SCALAR_SHARE:], w1_source[:, SCALAR_SHARE:])
        w2_rows = w2.rearrange("(p j) c -> p j c", j=PACK)
        w2_early = keep.tile([P, PACK, N // 2], F32, name="w2_early", tag="w1_raw_then_w2_raw")
        nc.sync.dma_start(w2_early[:], w2_rows[:, :, : N // 2])
        w1_codes = keep.tile([P, H], U32, name="w1_codes", align_bytes=64)
        w1_scale = keep.tile([P, H], U8, name="w1_scale", align_bytes=64)
        nc.vector.quantize_mx(w1_codes[:].bitcast(FP8X4), w1_scale[:], w1_bf[:])
        w2_late = keep.tile(
            [P, PACK, N // 2], F32, name="w2_late", tag="w1_bf_then_w2_raw", align_bytes=64
        )
        nc.sync.dma_start(w2_late[:], w2_rows[:, :, N // 2 :])
        ga_column = keep.tile([P, S // P], F32, name="ga_column", tag="picked_then_ga", align_bytes=64)
        with nc.allow_non_contiguous_dma(reason="one weight a partition"):
            nc.sync.dma_start(ga_column[:], ga[0].rearrange("(b p) -> p b", p=P))
        identity = keep.tile([P, P], F32, name="identity")
        make_identity(nc, identity[:])

        x_codes = keep.tile([P, S], U32, name="x_codes", align_bytes=64)
        halves = [slice(0, S // 2), slice(S // 2, S)]
        blocks = [slice(b * P, (b + 1) * P) for b in range(S // P)]
        x_parts = [halves[0], blocks[2], blocks[3]]
        for cols in x_parts:
            nc.vector.tensor_copy(
                x_codes[:, cols], x_table[:].bitcast(U32).indirect(entries(offs_sb, cols))
            )

        whole = slice(0, S)

        def first_product(acc, t, cols):
            nc.tensor.matmul_mx(
                acc[:, cols],
                lhsT=w1_codes[:, blocks[t]].bitcast(FP8X4),
                lhsT_scale=w1_scale[:, blocks[t]],
                rhs=x_codes[:, cols].bitcast(FP8X4),
                rhs_scale=x_scale[:, cols],
                start=True,
                stop=True,
            )

        y = [keep.tile([P, WIDE], F32, name="y%d" % t) for t in range(PACK)]

        y_banks = [[] for t in range(PACK)]

        def make_y(t, cols, at, copy):
            acc = bank(at)
            first_product(acc, t, cols)
            copy(y[t][:, cols], acc[:, cols])
            y_banks[t].append((cols, acc))

        make_y(0, x_parts[0], 0, nc.scalar.copy)
        make_y(1, halves[0], 1, nc.vector.tensor_copy)
        make_y(0, x_parts[1], 2, nc.scalar.copy)
        make_y(0, x_parts[2], 3, nc.scalar.copy)
        make_y(1, halves[1], 4, nc.vector.tensor_copy)
        make_y(2, whole, 5, nc.vector.tensor_copy)
        late_bank = bank(6)
        first_product(late_bank, 3, whole)
        y_banks[3] = [(cols, late_bank) for cols in halves]
        ga_bank = bank(7)
        for b, cols in enumerate(blocks):
            nc.tensor.matmul(
                ga_bank[:, cols],
                lhsT=ga_column[:, b : b + 1].to_broadcast([P, P]),
                rhs=identity[:],
                is_transpose=True,
                start=True,
                stop=True,
            )

        shared = dict(align_bytes=64)
        first = [
            keep.tile([P, S], F32, name="first%d" % t, tag="first%d" % t, **shared) for t in range(PACK)
        ]
        both = [keep.tile([P, S], F32, name="both%d" % t) for t in range(PACK - 1)]
        weighted = [
            keep.tile([P, S], F32, name="weighted%d" % t, tag="weighted%d" % t, **shared)
            for t in range(PACK - 1)
        ]
        h_all = keep.tile([P, PACK * S], F32, name="h_all")
        h_window = [
            keep.tile([P, WIDE if t < PACK - 1 else S], F32, name="h_window%d" % t)
            for t in range(PACK)
        ]
        far = keep.tile([P, PACK * S], F32, name="far")
        w2_scale = keep.tile([P, N], U8, name="w2_scale", align_bytes=64)

        def plane(tile, t, cols=whole):
            return tile[:, t * S + cols.start : t * S + cols.stop]

        def fetch_first(t):
            nc.scalar.activation(first[t][:], y[t][:].indirect(p1_sb[:]), COPY)

        def fetch_second(t):
            nc.vector.tensor_tensor(both[t][:], y[t][:].indirect(p2_sb[:]), first[t][:], ADD)

        def weigh(t, cols=whole):
            nc.vector.tensor_tensor(weighted[t][:, cols], both[t][:, cols], ga_bank[:, cols], MULT)

        def add_own(t, term, pieces=slice(None)):
            for cols, acc in y_banks[t][pieces]:
                nc.vector.tensor_tensor(h_window[t][:, cols], term[:, cols], acc[:, cols], ADD)

        def fetch_far(t, cols):
            nc.scalar.activation(plane(far, t, cols), h_window[t][:].indirect(entries(q1_sb, cols)), COPY)

        w2_bf = [keep.tile([P, N // 2, PACK], BF16, name="w2_bf0", tag="x_table_then_w2_bf", **shared)]

        def w2_part(u, cols):
            return (
                w2_bf[u][:, cols, :].rearrange("p (c i) t -> p c t i", i=4),
                (w2_early, w2_late)[u][:, :, cols].rearrange("p t (c i) -> p c t i", i=4),
            )

        def round_w2(u, cols):
            nc.gpsimd.tensor_scalar(*w2_part(u, cols), 1.0, 0.0, MULT, ADD)

        def quantise_w2(u):
            nc.vector.quantize_mx(
                w2_codes[:, halves[u]].bitcast(FP8X4),
                w2_scale[:, halves[u]],
                w2_bf[u][:, halves[0], :].rearrange("p n j -> p (n j)"),
            )

        round_w2(0, halves[0])
        for t in range(PACK - 1):
            fetch_first(t)
        nc.scalar.copy(y[3][:, whole], late_bank[:])
        fetch_first(3)
        second = keep.tile([P, S], F32, name="second")
        nc.scalar.activation(second[:], y[3][:].indirect(p2_sb[:]), COPY)

        def finish_plane(t, pieces=slice(None)):
            add_own(t, weighted[t], pieces)
            nc.sync.dma_start(plane(h_all, t), h_window[t][:, whole])
            fetch_far(t, whole)

        fetch_second(0)
        fetch_second(1)
        w2_bf.append(keep.tile([P, UNDER_WEIGHINGS + P, PACK], BF16, name="w2_bf1", tag="first1", **shared))
        round_w2(1, slice(0, UNDER_WEIGHINGS))
        weigh(0)
        weigh(1)
        finish_plane(0)
        add_own(1, weighted[1], slice(0, 1))
        fetch_second(2)
        both.append(keep.tile([P, S], F32, name="both3", tag="first2", **shared))
        for cols in halves:
            nc.gpsimd.tensor_tensor(both[3][:, cols], first[3][:, cols], second[:, cols], ADD)
        finish_plane(1, slice(1, 2))
        weigh(2)
        behind_rounded = w2_bf[1][:, UNDER_WEIGHINGS:, :].rearrange("p n j -> p (n j)").bitcast(F32)
        staged = [behind_rounded, plane(far, 2, halves[1])]
        nc.vector.tensor_tensor(staged[0], both[3][:, halves[0]], ga_bank[:, halves[0]], MULT)
        add_own(2, weighted[2])
        nc.gpsimd.tensor_scalar(plane(h_all, 2), h_window[2][:, whole], 1.0, 0.0, MULT, ADD)
        fetch_far(2, halves[0])
        nc.vector.tensor_tensor(staged[1], both[3][:, halves[1]], ga_bank[:, halves[1]], MULT)
        for u, (cols, acc) in enumerate(y_banks[3]):
            nc.vector.tensor_tensor(h_window[3][:, cols], staged[u], acc[:, cols], ADD)
        nc.vector.tensor_copy(plane(h_all, 3, halves[0]), h_window[3][:, halves[0]])
        nc.vector.tensor_copy(*w2_part(1, slice(UNDER_WEIGHINGS, N // 2)))
        w2_codes = keep.tile([P, N], U32, name="w2_codes", tag="first2", **shared)
        for u in range(2):
            quantise_w2(u)
        fetch_far(3, blocks[0])
        fetch_far(3, blocks[1])
        fetch_far(2, halves[1])
        nc.scalar.copy(plane(h_all, 3, halves[1]), h_window[3][:, halves[1]])
        fetch_far(3, blocks[2])
        fetch_far(3, blocks[3])

        out_rows = out.rearrange("(b p) n -> p b n", p=P)

        def by_fours(tile, cols):
            return tile[:].rearrange("p (t c i) -> p c t i", t=PACK, i=4)[:, cols.start // 4 : cols.stop // 4]

        z_bf = [keep.tile([P, P, PACK], BF16, name="z_bf%d" % b, align_bytes=64) for b in range(PACK)]
        groups = [blocks[0], blocks[1], halves[1]]
        z_codes = [
            keep.tile([P, g.stop - g.start], U32, name="z_codes%d" % g.start, align_bytes=64) for g in groups
        ]
        z_scale = [
            keep.tile([P, g.stop - g.start], U8, name="z_scale%d" % g.start, align_bytes=64) for g in groups
        ]

        def difference(b):
            nc.vector.tensor_tensor(
                z_bf[b][:].rearrange("p (c i) t -> p c t i", i=4),
                by_fours(h_all, blocks[b]),
                by_fours(far, blocks[b]),
                SUBTRACT,
            )

        def quantise_z(b, g, cols):
            nc.vector.quantize_mx(
                z_codes[g][:, cols].bitcast(FP8X4),
                z_scale[g][:, cols],
                z_bf[b][:].rearrange("p n t -> p (n t)"),
            )

        def second_product(acc, g, m, cols):
            nc.tensor.matmul_mx(
                acc,
                lhsT=w2_codes[:, blocks[m]].bitcast(FP8X4),
                lhsT_scale=w2_scale[:, blocks[m]],
                rhs=z_codes[g][:, cols].bitcast(FP8X4),
                rhs_scale=z_scale[g][:, cols],
                start=True,
                stop=True,
            )

        def finish_narrow(g, banks):
            for u, at in enumerate(banks):
                acc = bank(at)
                for n in range(2):
                    second_product(acc[:, blocks[n]], g, 2 * u + n, blocks[0])
                result = keep.tile([P, 2, P], F32, name="narrow%d_%d" % (g, u))
                nc.scalar.copy(result[:].rearrange("p m n -> p (m n)"), acc[:, halves[0]])
                nc.sync.dma_start(out_rows[:, 2 * u : 2 * u + 2, groups[g]], result[:])

        def finish_wide(m, pieces, copy):
            result = keep.tile([P, 2 * P], F32, name="wide%d" % m)
            for cols, at in pieces:
                acc = bank(at)
                second_product(acc[:, cols], 2, m, cols)
                copy(result[:, cols], acc[:, cols])
            nc.sync.dma_start(out_rows[:, m, groups[2]], result[:])

        difference(0)
        difference(1)
        quantise_z(0, 0, blocks[0])
        finish_narrow(0, (7, 0))
        difference(2)
        quantise_z(1, 1, blocks[0])
        finish_narrow(1, (1, 2))
        difference(3)
        quantise_z(2, 2, blocks[0])
        quantise_z(3, 2, blocks[1])
        finish_wide(0, [(blocks[0], 7), (blocks[1], 3)], nc.vector.tensor_copy)
        finish_wide(1, [(halves[0], 4)], nc.vector.tensor_copy)
        finish_wide(2, [(halves[0], 5)], nc.scalar.copy)
        finish_wide(3, [(halves[0], 6)], nc.vector.tensor_copy)
